import numpy as np, ml_dtypes
CORES = [40,42,43,45,46]
N = 5
BF = ml_dtypes.bfloat16
def gentries(a):
    return np.ascontiguousarray(a.reshape(8, 16, -1).transpose(0, 2, 1)).reshape(8, -1)
def gtable(e):
    e = np.asarray(e); return np.ascontiguousarray(e.reshape(8, -1, 16).transpose(0, 2, 1)).reshape(128, -1).astype(np.int32)
PL, D, P, T, H, S, Q4 = 4096, 1024, 128, 4, 2, 32, 1024
def entry(rng, *shape):
    return np.where(rng.random(shape) < 0.5, rng.integers(0, PL, shape), PL + rng.integers(0, D, shape))
def parts(rng):
    x = rng.integers(0, 64, (N, 8, 16, PL)); a = entry(rng, N, 8, 16, D); b = entry(rng, N, 8, 16, D); z = rng.integers(0, 64, (N, 8, 16, P))
    v = rng.integers(0, D, (N, 8, P)); p = rng.integers(0, D, (N, 8, P)); w = rng.integers(0, 256, (N, 8, 16)); h = rng.integers(100, 401, (N, 8, 16))
    return x, a, b, z, v, p, w, h
def pack(x, a, b, z, v, p, w, h):
    return {"xl": np.reshape(x, (N, 128, PL)).astype(np.float32).astype(BF), "vdir": np.reshape(a, (N, 128, D)).astype(np.int32), "pdir": np.reshape(b, (N, 128, D)).astype(np.int32),
            "z": np.reshape(z, (N, 128, P)).astype(np.float32).astype(BF), "vn": np.stack([gtable(e) for e in v]), "pn": np.stack([gtable(e) for e in p]),
            "wt": np.reshape(w, (N, 128, 1)).astype(np.int32), "th": np.reshape(h, (N, 128, 1)).astype(np.int32)}
def setup_inputs(rng):
    return pack(*parts(rng))
def setup_inputs_spread(rng):
    x, a, b, z, v, p, w, h = parts(rng)
    x = (np.exp2(6 * rng.random((N, 8, 1, PL))) * rng.random((N, 8, 16, PL))).astype(np.int64); z = (np.exp2(6 * rng.random((N, 8, 1, P))) * rng.random((N, 8, 16, P))).astype(np.int64)
    x = np.minimum(x, 63); z = np.minimum(z, 63)
    def uneven(n, *shape):
        r = rng.random(shape) ** 3
        return np.minimum((n * np.where(rng.random(shape) < 0.5, r, 1 - r)).astype(np.int64), n - 1)
    a = uneven(PL + D, N, 8, 16, D); b = uneven(PL + D, N, 8, 16, D); v = uneven(D, N, 8, P); p = uneven(D, N, 8, P)
    w = np.minimum((np.exp2(8 * rng.random((N, 8, 16))) * rng.random((N, 8, 16))).astype(np.int64), 255)
    h = np.minimum(np.exp2(10 * rng.random((N, 8, 16))).astype(np.int64) - 1, 1008); h[:, :, 3] = 1008; w[:, :, 3] = 255
    return pack(x, a, b, z, v, p, w, h)
def tips(rng, shape, hi, inner):
    e = hi * rng.integers(0, 2, shape); o = np.where(rng.random(shape) < 0.5, rng.choice(np.array(inner), shape), rng.integers(0, hi + 1, shape))
    return np.where(rng.random(shape) < 0.8, e, o)
def setup_inputs_ends(rng):
    m = rng.integers(0, 3, (N, 8, 1, PL)); x = 63 * np.where(m == 2, rng.integers(0, 2, (N, 8, 16, PL)), m)
    m = rng.integers(0, 3, (N, 8, 1, P)); z = 63 * np.where(m == 2, rng.integers(0, 2, (N, 8, 16, P)), m)
    top = PL + D - 1; w = 255 * rng.integers(0, 2, (N, 8, 16)); h = 1008 * rng.integers(0, 2, (N, 8, 16))
    a = tips(rng, (N, 8, 16, D), top, [PL - 1, PL, 1]); b = tips(rng, (N, 8, 16, D), top, [PL - 1, PL, 1])
    v = tips(rng, (N, 8, P), D - 1, [1, D - 2]); p = tips(rng, (N, 8, P), D - 1, [1, D - 2])
    for g in (0, 7):
        w[:, g] = 255; h[:, g, 0] = 0; h[:, g, 1] = 1008; h[:, g, 14] = 0; h[:, g, 15] = 1008
        for c in (0, D - 1):
            x[:, g, :, c] = 0; a[:, g, :, c] = top * rng.integers(0, 2, (N, 16)); b[:, g, :, c] = top * rng.integers(0, 2, (N, 16))
        for c in (Q4 - 2, 2 * Q4 - 2, 3 * Q4 - 2, PL - 2, PL - 1): x[:, g, :, c] = 63
        for i in (0, 1, P - 1): z[:, g, :, i] = 63
        for i in (2, P - 2): z[:, g, :, i] = 0
        for i, c in ((0, D - 1), (1, 0), (2, D - 1), (P - 2, 0), (P - 1, D - 1)): v[:, g, i] = c; p[:, g, i] = c
    return pack(x, a, b, z, v, p, w, h)
def setup_inputs_corners(rng):
    x, a, b, z, v, p, w, h = parts(rng); own = np.arange(D)[None, :]
    h = np.where(rng.random(h.shape) < 0.6, rng.choice(np.array([0, 1, 1007, 1008]), h.shape), h); w = np.where(rng.random(w.shape) < 0.5, rng.choice(np.array([0, 1, 255]), w.shape), w)
    for q in range(N):
        o = rng.permutation(8)
        for g in range(8):
            c = int(o[g])
            if c == 0:
                a[q, g] = rng.integers(0, PL, (16, D)); b[q, g] = rng.integers(0, PL, (16, D))
                k = rng.choice(np.array([0, 15]), P); e = a[q, g][k, v[q, g]]; m = np.arange(P) % 3 == 0
                z[q, g] = np.where(m[None, :], x[q, g][:, e], z[q, g])
            elif c == 1: a[q, g] = PL + rng.integers(0, D, (16, D)); b[q, g] = PL + rng.integers(0, D, (16, D))
            elif c == 2: a[q, g] = PL + rng.integers(0, D, (16, D)); b[q, g] = rng.integers(0, PL, (16, D))
            elif c == 3:
                a[q, g] = np.where(own % 2 == 0, PL + rng.integers(0, D, (16, D)), rng.integers(0, PL, (16, D)))
                b[q, g] = PL + 2 * rng.integers(0, D // 2, (16, D)) + 1; v[q, g] = 2 * rng.integers(0, D // 2, P)
            elif c == 4:
                a[q, g] = PL + own; b[q, g] = PL + own; b[q, g, 8:] = PL + (own + 1) % D
            elif c == 5:
                a[q, g] = rng.choice(np.array([0, PL - 1, PL, PL + D - 1]), (16, D)); b[q, g] = rng.choice(np.array([0, PL - 1, PL, PL + D - 1]), (16, D)); w[q, g] = 0
            elif c == 6:
                a[q, g] = PL + (D - 1) * rng.integers(0, 2, (16, D)); w[q, g] = 255
            else:
                p[q, g] = v[q, g]; v[q, g, 0] = 0; v[q, g, P - 1] = D - 1; p[q, g, 0] = D - 1; p[q, g, P - 1] = 0
    return pack(x, a, b, z, v, p, w, h)
def setup_inputs_crowd(rng):
    x, a, b, z, v, p, w, h = parts(rng)
    for q in range(N):
        for g in range(8):
            c, e = rng.permutation(D)[:P], rng.permutation(D)[:P]; s, t = int(rng.integers(0, D)), int(rng.integers(0, D))
            if g == 0: c[:] = s
            elif g == 1: e[:] = s
            elif g == 2: c[:] = s; e[:] = t
            elif g == 3: c[:] = s; c[P - 1] = (s + 1) % D
            elif g == 4: e[:] = s; e[0] = (s + 1) % D
            elif g == 5: c = rng.choice(np.array([0, D - 1]), P); e = rng.choice(np.array([0, D - 1]), P)
            elif g == 6 and q < N - 1:
                if q % 2 == 0: e[P - 1] = e[0]
                else: c[P - 1] = c[0]
            elif g == 7: c[:] = s; e[:] = t; z[q, g] = z[q, g, :, :1]
            v[q, g] = c; p[q, g] = e
    h[0] = 0; h[N - 1] = 0; h[N - 1, 6, 15] = 1
    x[1] = 56 + (x[1] >> 3); z[1] = 56 + (z[1] >> 3); h[1] = rng.integers(630, 801, (8, 16))
    x[2] = x[2] >> 3; z[2] = 30 * z[2] >> 6; h[2] = rng.integers(480, 761, (8, 16))
    m = 2 * int(rng.integers(10, 20)) + 1; j = rng.permutation(P)[:m]; k = rng.permutation(16)
    z[2, 5][:, j] = rng.integers(45, 52, (16, m)); h[2, 5, k[:5]] = rng.integers(480, 609, 5); h[2, 5, k[5:]] = rng.integers(820, 1009, 11)
    x[N - 1, 6, 0] = 63; z[N - 1, 6, 0] = rng.integers(0, 63, P); n = int(rng.integers(0, PL))
    a[N - 1, 6, 15, v[N - 1, 6, P - 1]] = n; z[N - 1, 6, :, P - 1] = x[N - 1, 6, :, n]
    return pack(x, a, b, z, v, p, w, h)
def setup_inputs_ties(rng):
    x, a, b, z, v, p, w, h = parts(rng)
    for q in range(N):
        few = q in (1, 3)
        for g in range(8):
            if g % 2 == 0:
                y = rng.integers(21 if few else 0, 41, (16, 1)); x[q, g] = y + 3 * rng.integers(0, 6, (1, PL)); z[q, g] = y + 3 * rng.integers(0, 8, (1, P))
                h[q, g] = rng.choice(np.array([0, 1, 48, 49, 96, 97, 144, 145]), 16)
                if few: h[q, g] = np.sum(y) + 48 * rng.integers(1, 6, 16) - rng.permutation(16) // 6
            else:
                x[q, g] = rng.integers(0, 64, (16, 8))[:, rng.integers(0, 8, PL)]
                v[q, g] = rng.permutation(D)[:P]; p[q, g] = rng.permutation(D)[:P]
                if g % 4 == 1: v[q, g, P - 1] = v[q, g, 0]
                else: p[q, g, P - 1] = p[q, g, 0]
                if few: x[q, g] = x[q, g] >> 2; z[q, g] = z[q, g] >> 2; h[q, g] = rng.integers(241, 301, 16)
    m = rng.permutation(3) + 1
    for i, q in ((0, 1), (1, 3)):
        z[q, 7, :, P - 1] = 62; k = rng.permutation(16)[int(m[i]):]; h[q, 7, k] = 1008
    return pack(x, a, b, z, v, p, w, h)
def check_inputs(d):
    bad = []
    for k, hi in (("xl", 63), ("vdir", PL + D - 1), ("pdir", PL + D - 1), ("z", 63), ("vn", D - 1), ("pn", D - 1), ("wt", 255), ("th", 1008)):
        e = np.asarray(d[k]).astype(np.float64)
        if not (np.min(e) >= 0 and np.max(e) <= hi): bad.append("range of " + k)
        elif not np.all(e == np.floor(e)): bad.append("whole numbers in " + k)
    return bad
def reference(xl, vdir, pdir, z, vn, pn, wt, th):
    X = xl.astype(np.float32).astype(np.int64).reshape(N, 8, 16, PL); Z = z.astype(np.float32).astype(np.int64).reshape(N, 8, 16, P)
    VD = vdir.astype(np.int64).reshape(N, 8, 16, D); PD = pdir.astype(np.int64).reshape(N, 8, 16, D)
    w = wt.astype(np.int64).reshape(N, 8, 16, 1); h = th.astype(np.int64).reshape(N, 8, 16, 1)
    v = np.stack([gentries(a) for a in vn]).astype(np.int64); p = np.stack([gentries(a) for a in pn]).astype(np.int64)
    A = np.zeros(N, np.int64); lower = np.tri(P, P, -1, dtype=bool)
    for t in range(T):
        if t > 0: v, p, Z = np.roll(v, 1, axis=0), np.roll(p, 1, axis=0), np.roll(Z, 1, axis=0)
        e = np.take_along_axis(VD, v[:, :, None, :], 3)
        for i in range(H):
            e = np.where(e >= PL, np.take_along_axis(PD if i % 2 == 0 else VD, np.maximum(e - PL, 0), 3), e)
        e = np.where(e >= PL, e - PL, e)
        x = np.take_along_axis(X, e.reshape(N, 8, 1, 16 * P), 3).reshape(N, 8, 16, 16, P)
        d = np.add.reduce(np.abs(x - Z[:, :, :, None, :]), axis=2)
        ks = np.argmin(d, axis=2)[:, :, None, :]
        xs = np.take_along_axis(x, ks[:, :, None], 3)[:, :, :, 0]
        u = np.add.reduce(w * Z, axis=2) & 4095
        n = S * np.arange(P) + (u & (S - 1))
        near = d < h + (A & 255)[:, None, None, None]
        np.put_along_axis(e, ks, n[:, :, None, :], 2)
        np.put_along_axis(X, n[:, :, None, :], (xs + Z) >> 1, 3)
        same = (v[..., :, None] == v[..., None, :]) | (p[..., :, None] == p[..., None, :])
        edits = ~np.any(same & lower, axis=-1)
        tov = np.where(near, e, PL + p[:, :, None, :]); top = np.where(near, PL + v[:, :, None, :], e)
        for q in range(N):
            for g in range(8):
                m = edits[q, g]
                VD[q, g][:, v[q, g][m]] = tov[q, g][:, m]; PD[q, g][:, p[q, g][m]] = top[q, g][:, m]
        A = np.add.reduce((1 - near.astype(np.int64)).reshape(N, -1), axis=1)
        p, v = v, ((u * u >> 5) + 37 * v) & (D - 1)
        Z = np.abs(Z - xs)
    yx = X[..., :Q4] + 64 * X[..., Q4:2 * Q4] + 4096 * X[..., 2 * Q4:3 * Q4] + 262144 * X[..., 3 * Q4:]
    return {"yx": yx.reshape(N, 128, Q4).astype(np.float32), "yvd": VD.reshape(N, 128, D).astype(np.float32), "ypd": PD.reshape(N, 128, D).astype(np.float32),
            "yz": Z.reshape(N, 128, P).astype(np.float32).astype(BF), "yvp": (D * p + v).astype(np.float32)}

@@ -1,0 +1,651 @@
+from concourse.bass import DstId, RemoteDMATransfer
+from concourse.mybir import AluOpType as OP, ActivationFunctionType as AF, AxisListType as AX
+
+F32, BF, F16, I32, U16 = "float32", "bfloat16", "float16", "int32", "uint16"
+NT = 4
+BIG = 8192.0
+LV = (24, 24, 24, 24)
+XS = 24
+ONV = ("mob", "cnt", "zt", "ev", "z192", "aq", "ac", "tha")
+DEC = ((2, 1), (3, 1), (2, 1), (3, 1), (4, 0), (5, 0), (4, 0), (5, 0))
+GAT, SCA, HOP, FAR = 1.56, 3.5, 70.0, 2000.0
+
+
+def _sb(n, d):
+    return ("sbuf", [128, n], d)
+
+
+SCRATCH = {
+    "rv": _sb(1024, I32), "rp": _sb(1024, I32), "vd": _sb(1160, F32), "pd": _sb(1160, F32),
+    "ov": _sb(1160, F32), "op_": _sb(1160, F32), "ox": _sb(1024, F32), "xw": _sb(6144, BF),
+    "vni": _sb(8, I32), "pni": _sb(8, I32), "wi": _sb(4, I32), "wn": _sb(4, I32), "thi": _sb(128, I32),
+    "thf": _sb(128, F32), "th16": _sb(128, F32), "tha": _sb(128, F32),
+    "ci": _sb(16, I32), "cf": _sb(16, F32), "l16": _sb(16, F32), "m16": _sb(16, F32), "sg": _sb(16, F32),
+    "pw": _sb(16, F32), "pw2": _sb(16, F32), "two": _sb(16, F32), "c16": _sb(8, F32), "jj": _sb(8, F32),
+    "j32": _sb(8, F32), "j16": _sb(8, F32), "dump": _sb(16, F32), "bci": _sb(8, I32), "bc": _sb(8, U16),
+    "x144": _sb(144, F32), "g128": _sb(128, F32), "bs": _sb(144, BF), "bw0": _sb(144, BF), "bw1": _sb(144, BF),
+    "bk": _sb(144, BF), "blk": _sb(128, BF), "b16": _sb(8, BF), "kc": _sb(128, BF),
+    "rs": _sb(128, F32), "ones": _sb(128, BF), "onef": _sb(128, F32), "ib": _sb(128, BF),
+    "iff": _sb(128, F32), "nif": _sb(128, F32), "nbig": _sb(256, BF), "sc3": _sb(384, BF), "u01": _sb(128, BF),
+    "c48": _sb(64, BF), "bigc": _sb(8, BF), "w2": _sb(256, BF), "dk": _sb(2048, F16), "ee": _sb(2048, BF),
+    "ft": _sb(1040, BF), "iot": _sb(4096, F32),
+    "eq": ("sbuf", [128, 8, 8, 16], BF), "vl": _sb(64, U16),
+    "om": _sb(16, F32), "osc": _sb(16, U16), "nl": _sb(8, U16), "nx": _sb(8, U16),
+    "o1": _sb(128, U16), "o2": _sb(128, U16), "o3": _sb(128, U16), "r1": _sb(128, F32), "r2": _sb(128, F32),
+    "g2": _sb(2048, F16), "g3": _sb(2048, F16), "xg": _sb(2048, BF), "ab": _sb(2048, BF), "zt": _sb(128, BF),
+    "ff": _sb(128, F32), "e4": _sb(128, F32), "nme": _sb(128, F32), "pm": _sb(128, F32),
+    "near": _sb(128, BF), "ge": _sb(128, BF), "key": _sb(128, F32), "t1": _sb(128, F32), "ep": _sb(128, F32), "rr": _sb(256, F32),
+    "oh": _sb(128, BF), "kl": _sb(8, U16), "df": _sb(128, BF), "tt": _sb(128, BF), "z192": _sb(128, BF),
+    "ac": _sb(8, F32), "aq": _sb(8, BF), "iw": _sb(64, I32), "yl": _sb(16, U16), "ya": _sb(128, F32), "yb": _sb(128, F32),
+    "zi": _sb(128 * NT, BF), "zo": _sb(128 * NT, BF), "fi": _sb(264 * NT, BF), "fo": _sb(264 * NT, BF),
+    "mo": _sb(24 * NT, F32), "mn": _sb(24 * NT, F32), "ml": _sb(24 * NT, F32),
+}
+for _t in range(8):
+    SCRATCH["b%d" % _t] = ("psum", [128, 512], F32)
+
+NDMA = 24
+SEMAPHORES = (["cV", "cS", "cP", "cG", "sent", "aw"] + ["d%d" % i for i in range(NDMA)]
+              + [a + str(t) for a in ("az", "an", "al", "af") for t in range(1, NT)])
+
+
+PUSH = {x.split(":")[0]: 100 * int(x.split(":")[1]) for x in """
+sYvni.1:900 sYrv0.1:800 sYrv1.1:700 sYrp0.1:600 sYrp1.1:500 sYxa.1:400 sSpni.1:900 sSwi.1:800 sSz.1:700 sSthi.1:600
+Vzt6.1:140 Vxg1.1:336 Pfoe2.2:-297 Seq02.1:-268 Vov13.1:-189 Sr200.1:96 Pzt5.1:-193 Vov22.1:-120 Vov.1:22 Vsq.1:169 Vu12.1:122 Szo.1:261 sVblk.1:-34 Vvl.1:184 sGg128.1:105 sVxe.4:-24 sVs1.1:-16 sPfoe4.2:-326 Spb33.1:-65 sVtwo.1:-32 sVci2.1:6 Vvw.1:129 sVsq.1:116 Pnear4.1:34 sSiff.1:-209 sSeq55.1:-113 Seq22.1:61 sGiot7.1:-87 sVdk.6:-80 Vop24.1:11 Soh0.1:-20 Vnl.1:50 sVbs.1:41 sVdk.11:-52 sGl16.1:38 Vff.1:-41 sGci0.1:162 sGkc.1:-54 sGiot5.1:-35 Vmob.1:74 Vxg0.1:27 Vz92.1:-93 sSdumpa.1:-97 sSbk.1:-153 eVya.1:90 Vs1.1:115 Vkl5.1:-16 Seq63.1:-126 Vui5.1:38 sPfie3.2:-58 sVxe.2:-15 sVj32.1:60 Vo300.1:-5 Sxgs.1:59 sGee3.1:-56 Pnif1.2:-62 sVmoc.1:115 Vmoc.1:53 Pib4.1:-125 sVwc.1:-56 sVjj.1:-9 Sg21s.1:130 Seq53.1:46 Pnif0.2:-129 Seq12.1:59 Seq32.1:34 Vxe2.1:18 sSth166.1:-76 sSeq43.1:-70 sVmo.1:165 sVme.1:78 sSft.10:-185 sVfic7.1:-7 Vov02.1:-185 Vo200.1:-17 sSfio.1:87 Vnx.1:-73 sVdk.7:24 sGiot4.1:-92 Pbw15.1:-121 Sr1.1:-89 sGiot0.1:-18 sVm.1:-5 Pbigc7.1:-12 sVm6.1:65 sVpd0.1:-49 sVgb.1:60 sPfoe4.4:38 Vg30v.1:18 sVee2.1:-7 ePib4.1:-15 sVdk.10:-52 Vnme.1:51 sVpd0.2:-42 Vtt.1:-90 sVenc11.2:-19 Spb44.2:15 sGbci.1:-50 Pw24.2:-68 sVdk.15:-20 sSnif.1:-30 Vpmin6.1:-24 Pfoo3.2:45 Srr14.1:75 sVee0.1:-10 sSeq02.1:-20 Sab24.1:5 Pzt4.1:40 Vg20v.1:-10 Vom7.1:25 sPbigc7.2:40 Vg31v.1:40
+""".split()}
+
+
+def planner(ops):
+    n = len(ops)
+    lastw, readers, bank = {}, {}, {}
+    pre = [dict() for _ in ops]
+    sends = {o["tag"]: i for i, o in enumerate(ops) if o["kind"] == "r"}
+    for i, o in enumerate(ops):
+        def dep(j, raw):
+            same = ops[j]["q"] == o["q"] and ops[j]["kind"] == "c" and o["kind"] == "c"
+            pre[i][j] = max(pre[i].get(j, 0), ops[j]["lat"] + (HOP if raw or not same else 0))
+        if o["kind"] == "a":
+            dep(sends[o["tag"]], True)
+        for k in o["r"]:
+            if k in lastw:
+                dep(lastw[k], True)
+        for k in o["w"]:
+            for j in readers.get(k, []):
+                dep(j, True)
+            if k in lastw:
+                dep(lastw[k], False)
+        for k in o["b"]:
+            if k in bank:
+                dep(bank[k], False)
+            bank[k] = i
+        for k in o["r"]:
+            readers.setdefault(k, []).append(i)
+        for k in o["w"]:
+            lastw[k] = i
+            readers[k] = []
+        pre[i].pop(i, None)
+    suc = [[] for _ in ops]
+    for i in range(n):
+        for j in pre[i]:
+            suc[j].append(i)
+    dur = [o["dur"] for o in ops]
+    que = [o["q"] if o["kind"] != "a" else "A" for o in ops]
+
+    def tails(order, after):
+        tail = [0.0] * n
+        for i in reversed(order):
+            t = ops[i]["lat"]
+            for j in suc[i]:
+                t = max(t, pre[j][i] + dur[j] + tail[j])
+            if after.get(i) is not None:
+                t = max(t, dur[after[i]] + tail[after[i]])
+            tail[i] = t
+        return tail
+
+    def plan(tail):
+        wait = [len(p) for p in pre]
+        rdy = [0.0] * n
+        pool = {q: [] for q in set(que)}
+        free = {q: 0.0 for q in pool}
+        for i in range(n):
+            if not wait[i]:
+                pool[que[i]].append(i)
+        order, after, last, span = [], {}, {}, 0.0
+        while len(order) < n:
+            t, q = min((max(free[q], min(rdy[i] for i in p)), q) for q, p in pool.items() if p)
+            p = pool[q]
+            x = max((i for i in p if rdy[i] <= t), key=lambda i: tail[i])
+            best = None
+            for y in p:
+                if t < rdy[y] < t + dur[x] and tail[y] > tail[x]:
+                    gain = t + dur[x] + dur[y] + tail[y] - max(rdy[y] + dur[y] + tail[y], rdy[y] + dur[y] + dur[x] + tail[x])
+                    if gain > 0 and (best is None or gain > best[0]):
+                        best = (gain, y)
+            if best:
+                fit = [i for i in p if rdy[i] <= t and t + dur[i] <= rdy[best[1]]]
+                x = max(fit, key=lambda i: tail[i]) if fit else best[1]
+            p.remove(x)
+            e = max(t, rdy[x]) + dur[x]
+            if q != "A":
+                free[q] = e
+                if q in last:
+                    after[last[q]] = x
+                last[q] = x
+            order.append(x)
+            span = max(span, e + ops[x]["lat"])
+            for j in suc[x]:
+                rdy[j] = max(rdy[j], e + pre[j][x])
+                wait[j] -= 1
+                if not wait[j]:
+                    pool[que[j]].append(j)
+        return span, order, after
+
+    tail = tails(plan([0.0] * n)[1], {})
+    return lambda push: plan([x + push.get(o["cls"], 0) for x, o in zip(tail, ops)])
+
+
+def arrange(ops):
+    order = planner(ops)(PUSH)[1]
+    return [ops[i] for i in order if ops[i]["kind"] == "a"] + [ops[i] for i in order if ops[i]["kind"] != "a"]
+
+
+def emit(g, T, ops):
+    Q = {"V": g.vector, "S": g.scalar, "P": g.tensor, "G": g, "Y": g.sync}
+    lastw, readers, bank, deps = {}, {}, {}, []
+    for i, o in enumerate(ops):
+        d = set()
+        own = o["q"] if o["kind"] == "c" else None
+        for k in o["r"]:
+            if k in lastw:
+                d.add(lastw[k])
+        for k in o["w"]:
+            d.update(readers.get(k, []))
+            if k in lastw and (ops[lastw[k]]["kind"] != "c" or ops[lastw[k]]["q"] != own):
+                d.add(lastw[k])
+        for k in o["b"]:
+            if k in bank and ops[bank[k]]["q"] != own:
+                d.add(bank[k])
+            bank[k] = i
+        for k in o["r"]:
+            readers.setdefault(k, []).append(i)
+        for k in o["w"]:
+            lastw[k] = i
+            readers[k] = []
+        d.discard(i)
+        deps.append(d)
+    know = {q: {} for q in Q}
+    done = []
+    need = []
+    for i, o in enumerate(ops):
+        kn = know[o["q"]] if o["kind"] != "a" else {}
+        mine = []
+        for j in sorted(deps[i], reverse=True):
+            key = ops[j]["q"] if ops[j]["kind"] == "c" else ("x", j)
+            if kn.get(key, -1) >= j:
+                continue
+            mine.append(j)
+            for k2, v2 in done[j].items():
+                if kn.get(k2, -1) < v2:
+                    kn[k2] = v2
+        need.append(mine)
+        dn = dict(kn)
+        dn[o["q"] if o["kind"] == "c" else ("x", i)] = i
+        done.append(dn)
+    awaited = set(j for m in need for j in m)
+    count = {q: 0 for q in Q}
+    at = {}
+    nd = [0]
+    sent = [0]
+    open_ = {}
+    for i, o in enumerate(ops):
+        if o["kind"] == "a":
+            at[i] = (o["sem"], o["n"])
+            open_[i] = at[i]
+            continue
+        q = Q[o["q"]]
+        for j in need[i]:
+            q.wait_ge(at[j][0], at[j][1])
+            open_.pop(j, None)
+        ins = o["f"]()
+        if o["kind"] == "c":
+            if i in awaited:
+                count[o["q"]] += 1
+                s = T.sem["c" + o["q"]]
+                ins.then_inc(s, 1)
+                at[i] = (s, count[o["q"]])
+        elif o["kind"] == "d":
+            s = T.sem["d%d" % nd[0]]
+            nd[0] += 1
+            ins.then_inc(s, 16)
+            at[i] = (s, 16)
+            open_[i] = at[i]
+        else:
+            sent[0] += o["n"]
+    g.wait_ge(T.sem.sent, sent[0])
+    for s, n in open_.values():
+        g.wait_ge(s, n)
+
+
+def rank_program(g, core, T, topo):
+    rank = T.rank_of(core)
+    if rank is None:
+        return
+    N = len(T.cores)
+    nxt, nx2, prv, pr2 = (T.cores[(rank + k) % N] for k in (1, 2, -1, -2))
+    ops, sect, seen = [], ["s"], {}
+    V, S, P = g.vector, g.scalar, g.tensor
+
+    def op(q, f, r=(), w=(), b=(), kind="c", n=0, sem=None, dur=64.0, lat=0.0, tag=None):
+        nm = (list(w) + [tag or ""] + list(r))[0 if w else (0 if tag else 1) if (tag or r) else 0]
+        for a in ("vl", "fo", "fi", "mo", "zo", "z", "m", "f", "mn", "ml", "fic", "foc", "foe", "foo", "fie", "fio"):
+            if nm[:len(a)] == a and nm[len(a):len(a) + 1].isdigit():
+                nm = a + nm[len(a) + 1:]
+        nm = sect[0] + q + nm + "".join(str(x) for x in b)
+        seen[nm] = seen.get(nm, 0) + 1
+        ops.append({"cls": nm + "." + str(seen[nm]), "q": q, "f": f, "r": list(r), "w": list(w), "b": list(b), "kind": kind, "n": n, "sem": sem,
+                    "dur": dur, "lat": lat, "tag": tag})
+
+    def els(a):
+        m = 1
+        for x in a.shape[1:]:
+            m *= x
+        return m
+
+    def ind(win, off):
+        return (win.indirect(off), 16 * els(off))
+
+    def vop(make, out, a, r, w, b, f):
+        if isinstance(out, tuple):
+            out, dur = out[0], 50.0 + SCA * out[1]
+        elif isinstance(a, tuple):
+            a, dur = a[0], 50.0 + GAT * a[1]
+        else:
+            dur = max(64.0, f * els(out))
+        op("V", lambda: make(out, a), r, w, b, dur=dur)
+
+    def ts(out, in0, s1, s2, o0, o1, r, w, b=(), f=1.0):
+        if o1 is None:
+            vop(lambda o, a: V.tensor_scalar(o, a, s1, None, o0), out, in0, r, w, b, f)
+        else:
+            vop(lambda o, a: V.tensor_scalar(o, a, s1, s2, o0, o1), out, in0, r, w, b, f)
+
+    def tt(out, a, c, o, r, w, b=()):
+        vop(lambda x, y: V.tensor_tensor(x, y, c, o), out, a, r, w, b, 1.0 if b else 2.0)
+
+    def cp(out, a, r, w, b=(), f=1.0):
+        vop(lambda x, y: V.tensor_copy(x, y), out, a, r, w, b, f)
+
+    def ms(out, c, w, r=(), f=0.5):
+        op("V", lambda: V.memset(out, c), r, w, dur=max(64.0, f * els(out)))
+
+    def act(out, a, func, r, w, b=(), bias=0.0, scale=1.0, acc=None):
+        dur = 65.0 + els(out)
+        if isinstance(a, tuple):
+            a, dur = a[0], 65.0 + GAT * a[1]
+        op("S", lambda: S.activation(out, a, func, bias=bias, scale=scale, accum_out=acc), r, w, b, dur=dur)
+
+    def aff(name, out, a, r, w, b=(), bias=0.0, scale=1.0, f=1.0):
+        if name in ONV:
+            ts(out, a, scale, bias, OP.mult, OP.add, r, w, b, f)
+        else:
+            act(out, a, AF.Identity, r, w, b, bias=bias, scale=scale)
+
+    def mm(out, l, rh, st, sp, r, bk, f=1.0):
+        op("P", lambda: P.matmul(out, l, rh, st, sp), r, (), [bk], dur=10.0 + 0.5 * f * max(min(64, els(l)), els(rh)))
+
+    def join(k):
+        part_ = ops[-k:]
+        del ops[-k:]
+        op("P", lambda: [o["f"]() for o in part_][-1], sorted(set(x for o in part_ for x in o["r"])), (), part_[0]["b"],
+           dur=sum(o["dur"] for o in part_))
+
+    def iota(out, pat, base, cm, w, fl=True):
+        if fl:
+            op("G", lambda: g.iota(out, pat, base, cm, allow_small_or_imprecise_dtypes=True), (), w, dur=130.0 + 2 * els(out))
+        else:
+            op("G", lambda: g.iota(out, pat, base, cm), (), w, dur=130.0 + 2 * els(out))
+
+    def asel(out, a, pat, c, base, cm, r, w):
+        op("G", lambda: g.affine_select(out, a, pat, c, 0.0, base, cm), r, w, dur=170.0 + 2 * els(out))
+
+    def dma(q, out, a, r, w, kb=0):
+        e = {"Y": g.sync, "S": S, "G": g}[q]
+        op(q, lambda: e.dma_start(out, a), r, w, kind="d", dur=60.0 + 4.0 * kb, lat=2000.0)
+
+    def eng(a, c):
+        return len(topo.engines(a, c))
+
+    def send(src, dests, r, tag):
+        trs, n = [], 0
+        share = len(dests)
+        for i, (c, dst, sem) in enumerate(dests):
+            es = topo.engines(core, c)
+            k = len(es) // share
+            m = sum(1 << e for e in es[i * k:(i + 1) * k])
+            rid, pid = topo.addr(c)[:2]
+            trs.append((c, dst, sem, m, rid, pid))
+            n += k
+        if share == 1:
+            c, dst, sem, m, rid, pid = trs[0]
+            op("G", lambda: g.remote_dma(dst, src, sem, T.sem.sent, pid, rid, m), r, kind="r", n=n, dur=600.0, lat=FAR - 600.0, tag=tag)
+        else:
+            op("G", lambda: g.remote_dma_fused(
+                [RemoteDMATransfer(dst_ids=[DstId(rid=x[4], pnc=x[5])], dma_engine_mask=x[3], remote_sem=x[2], src=src, dst=x[1])
+                 for x in trs], local_sem=T.sem.sent), r, kind="r", n=n, dur=600.0, lat=FAR - 600.0, tag=tag)
+
+    def arrive(sem, n, w, tag):
+        op("G", None, (), w, kind="a", n=n, sem=sem, dur=0.0, tag=tag)
+
+    B = [T["b%d" % i] for i in range(8)]
+
+    def part(buf, width):
+        return lambda t, a=0, e=width, s=1: buf[:, width * t + a:width * t + e:s] if s > 1 else buf[:, width * t + a:width * t + e]
+
+    ZI, ZO, FI, FO, MO, ML = part(T.zi, 128), part(T.zo, 128), part(T.fi, 264), part(T.fo, 264), part(T.mo, 24), part(T.ml, 24)
+    mn_ = part(T.mn, 24)
+
+    def MN(t, a=0, e=24):
+        return MO(0, a, e) if t == 0 else mn_(t, a, e)
+
+    MNk = [["mo0a", "mo0b", "mo0c"]] + [["mn%d" % t] * 3 for t in range(1, NT)]
+    IW = {k: T.iw[:, 8 * i:8 * i + 8] for i, k in enumerate(("ui", "u12", "m5", "sq", "q5", "v37", "s1", "vw"))}
+    arrive(T.sem.aw, eng(nxt, core), ["wn"], "w")
+    for t in range(1, NT):
+        arrive(T.sem["az%d" % t], eng(prv, core), ["z%d" % t], "z%d" % (t - 1))
+        arrive(T.sem["af%d" % t], eng(prv, core), ["fic%d" % t, "fie%d" % t, "fio%d" % t], "f%d" % (t - 1))
+        arrive(T.sem["an%d" % t], eng(prv, core) // (2 if t < NT - 1 else 1), ["mn%d" % t], "m%d" % t)
+        arrive(T.sem["al%d" % t], eng(prv, core) if t == 1 else eng(pr2, core) // 2, ["ml%d" % t], "m%d" % (t - 1))
+
+    dma("Y", T.vni[:], T.vn[:], (), ["vni"])
+    dma("S", T.pni[:], T.pn[:], (), ["pni"])
+    dma("S", T.wi[:, 0:1], T.wt[:], (), ["wi"])
+    dma("S", ZI(0), T.z[:], (), ["z0"])
+    dma("S", T.thi[0:1, :], T.th[:], (), ["thi"])
+    for raw, src, k in ((T.rv, T.vdir, "rv"), (T.rp, T.pdir, "rp")):
+        for h in range(2):
+            dma("Y", raw[:, 512 * h:512 * h + 512], src[:, 512 * h:512 * h + 512], (), [k + str(h)], 256)
+    dma("Y", T.xw[:, 0:1024], T.xl[:, 0:1024], (), ["xa"], 256)
+    dma("Y", T.xw[:, 1024:4096], T.xl[:, 1024:4096], (), ["xb"], 768)
+
+    pm, gb, me, mo, wc, w0, w1 = (T.cf[:, i:i + 1] for i in range(7))
+    ms(T.ones[:], 1.0, ["ones"])
+    iota(T.ci[:, 0:1], [[0, 1]], 0, 1, ["ci0"], False)
+    iota(T.l16[:], [[1, 16]], 0, 0, ["l16"])
+    asel(T.ib[:], T.ones[:], [[-1, 128]], OP.is_equal, 0, 1, ["ones"], ["ib"])
+    iota(T.c16[:], [[16, 8]], 0, 0, ["c16"])
+    iota(T.x144[:], [[1, 144]], -15, 0, ["x144"])
+    iota(T.g128[:], [[16, 8], [0, 16]], 0, 0, ["g128"])
+    asel(T.u01[:], T.ones[:], [[-1, 128]], OP.is_ge, 0, 1, ["ones"], ["u01"])
+    iota(T.kc[:], [[0, 8], [1, 16]], 0, 0, ["kc"])
+    iota(T.bci[:], [[16, 8]], 15, 0, ["bci"], False)
+    IOT = ["iot%d" % i for i in range(8)]
+    for i in range(8):
+        if i in (1, 2):
+            act(T.iot[:, 512 * i:512 * i + 512], T.iot[:, 0:512], AF.Identity, ["iot0"], [IOT[i]], bias=512.0 * i)
+        else:
+            iota(T.iot[:, 512 * i:512 * i + 512], [[1, 512]], 4096 + 512 * i, 0, [IOT[i]])
+    for q in range(4):
+        ms(T.ee[:, 512 * q:512 * q + 512], -1.0, ["ee%d" % q])
+        asel(T.ee[:, 512 * q:512 * q + 512], T.ee[:, 512 * q:512 * q + 512], [[-1, 32], [0, 16]], OP.is_equal, -32 * q, 1, ["ee%d" % q], ["ee%d" % q])
+        ms(T.xw[:, 4096 + 512 * q:4608 + 512 * q], 0.0, ["xe"])
+    for q in range(2):
+        cp(T.xw[:, 4096 + 1024 * q:5120 + 1024 * q:2], T.xw[:, 512 * q:512 * q + 512], ["xa", "xe"], ["xe2"], f=0.5)
+    ms(T.ft[:, 0:2], -1.0, ["ft"])
+    ms(T.two[:], 2.0, ["two"])
+    ts(T.ci[:, 1:2], T.ci[:, 0:1], 15, None, OP.bitwise_and, None, ["ci0"], ["ci1"])
+    ts(T.ci[:, 2:3], T.ci[:, 0:1], 16, None, OP.bitwise_and, None, ["ci0"], ["ci2"])
+    ms(T.vd[:, 0:1], 4096.0, ["vd0"])
+    cp(pm, T.ci[:, 1:2], ["ci1"], ["pm_"])
+    ms(T.pd[:, 0:1], 4096.0, ["pd0"])
+    ts(T.m16[:], T.l16[:], pm, None, OP.is_equal, None, ["l16", "pm_"], ["m16"])
+    ts(me, T.ci[:, 2:3], 0.0, None, OP.is_equal, None, ["ci2"], ["me"])
+    ts(T.sg[:], T.m16[:], -2.0, 1.0, OP.mult, OP.add, ["m16"], ["sg"])
+    ts(mo, T.ci[:, 2:3], 0.0, None, OP.is_gt, None, ["ci2"], ["mo"])
+    tt(gb, T.ci[:, 0:1], T.ci[:, 1:2], OP.subtract, ["ci0", "ci1"], ["gb"])
+    for l in range(10):
+        act(T.ft[:, 1 + 2 ** l:1 + 2 ** (l + 1)], T.ft[:, 1:1 + 2 ** l], AF.Copy, ["ft", "sg"], ["ft"], scale=T.sg[:, l:l + 1])
+    ts(T.nbig[:, 0:128], T.ib[:], -BIG, None, OP.mult, None, ["ib"], ["nbig"], f=0.5)
+    ms(T.bigc[:], BIG, ["bigc"])
+    ts(ML(0, 0, 8), T.vni[:], 1.0, None, OP.add, None, ["vni"], ["ml0"])
+    ts(ML(0, 8, 16), T.pni[:], 1.0, None, OP.add, None, ["pni"], ["ml0"])
+    ts(T.jj[:], T.c16[:], pm, None, OP.add, None, ["c16", "pm_"], ["jj"])
+    ts(T.bs[:], T.x144[:], gb, None, OP.is_equal, None, ["x144", "gb"], ["bs"])
+    cp(w0, T.wi[:, 0:1], ["wi"], ["w0"])
+    ts(T.j32[:], T.jj[:], 32.0, None, OP.mult, None, ["jj"], ["j32"])
+    ts(T.bw0[:], T.bs[:], w0, None, OP.mult, None, ["bs", "w0"], ["bw0"], f=0.5)
+    send(T.wi[:, 0:1], [(prv, T.wn[:, 0:1], T.sem.aw)], ["wi"], "w")
+    for k in range(16):
+        ts(T.dk[:, 128 * k:128 * k + 128], T.ib[:], T.m16[:, k:k + 1], None, OP.mult, None, ["ib", "m16"], ["dk"], f=0.5)
+    ts(T.blk[:], T.g128[:], gb, None, OP.is_equal, None, ["g128", "gb"], ["blk"])
+    op("V", lambda: V.tensor_tensor_scan(T.pw[:], T.two[:], T.ones[:, 0:16], 0.5, OP.mult, OP.mult), ["two", "ones"], ["pw"])
+    ms(T.c48[:], 48.0, ["c48"])
+    ms(T.pw[:, 10:11], -4096.0, ["pwa"], ["pw"])
+    ms(T.pw[:, 11:12], -1024.0, ["pwb"], ["pw"])
+    ms(T.pw[:, 12:13], 1.0, ["pwc"], ["pw"])
+    ms(T.pw[:, 13:16], 0.0, ["pwd"], ["pw"])
+    ts(T.b16[:], T.blk[:, 0:128:16], 16.0, None, OP.mult, None, ["blk"], ["b16"])
+    tt(T.pw2[:], T.pw[:], T.m16[:], OP.mult, ["pw", "pwa", "pwb", "pwc", "pwd", "m16"], ["pw2"])
+    ms(T.onef[0:1, :], 1.0, ["onef"], f=1.0)
+    op("V", lambda: V.tensor_reduce(wc, T.pw2[:], AX.X, OP.add), ["pw2"], ["wc"])
+    ts(T.thf[0:1, :], T.thi[0:1, :], 16.0, None, OP.mult, None, ["thi"], ["thf"])
+    ts(T.w2[:, 0:128], T.blk[:], wc, None, OP.mult, None, ["blk", "wc"], ["w2"], f=0.5)
+    ts(T.w2[:, 128:256], T.blk[:], wc, 0.5, OP.mult, OP.mult, ["blk", "wc"], ["w2"], f=0.5)
+    act(T.nbig[:, 128:256], T.ib[:], AF.Copy, ["ib"], ["pbig"], scale=BIG)
+    act(T.nif[:], T.ib[:], AF.Copy, ["ib"], ["nif"], scale=-1.0)
+    act(T.iff[:], T.ib[:], AF.Copy, ["ib"], ["iff"])
+    act(T.j16[:], T.jj[:], AF.Copy, ["jj"], ["j16"], scale=16.0)
+    act(T.bk[:], T.bs[:], AF.Copy, ["bs", "pm_"], ["bk"], scale=pm)
+    act(T.dump[:, 0:8], T.jj[:], AF.Identity, ["jj"], ["dumpa"], bias=1025.0)
+    act(T.dump[:, 8:16], T.jj[:], AF.Identity, ["jj"], ["dumpb"], bias=1025.0)
+    mm(B[6][:, 0:128], T.onef[0:1, :], T.thf[0:1, :], True, True, ["onef", "thf"], 6, 4)
+    act(T.tha[:], B[6][:, 0:128], AF.Copy, [], ["tha"], [6])
+    act(T.th16[:], B[6][:, 0:128], AF.Identity, [], ["th16"], [6], bias=790528.0)
+    ts(T.rs[:], T.kc[:], 0.0, 65536.0, OP.is_equal, OP.mult, ["kc"], ["rs"])
+    cp(T.bc[:], T.bci[:], ["bci"], ["bc"])
+    cp(w1, T.wn[:, 0:1], ["wn"], ["w1"])
+    ts(T.bw1[:], T.bs[:], w1, None, OP.mult, None, ["bs", "w1"], ["bw1"], f=0.5)
+    for i, s in enumerate((64.0, 4096.0, 262144.0)):
+        ts(T.sc3[:, 128 * i:128 * i + 128], T.ib[:], s, None, OP.mult, None, ["ib"], ["sc3"], f=0.5)
+
+    def encode(raw, tab, k, h, b0):
+        rk = "r" + k[0] + str(h)
+        ts(B[b0][:], raw[:, 512 * h:512 * h + 512], 4096.0, 0.0, OP.subtract, OP.max, [rk], ["enc%d" % b0], [b0])
+        tt(tab[:, 1 + 512 * h:513 + 512 * h], raw[:, 512 * h:512 * h + 512], B[b0][:], OP.add, [rk, "enc%d" % b0], [k], [b0])
+
+    def chain(s):
+        z, zk = (ZI, "z0") if s == 0 else (ZO, "zo%d" % (s - 1))
+        zs = max(s - 1, 0)
+        bw, bwk = (T.bw0, "bw0") if s == 0 else (T.bw1, "bw1")
+        vo, vk = (ML(0, 0, 8), "ml0") if s == 0 else (MN(s - 1, 0, 8), MNk[s - 1][0])
+        m, bk = "mo%d" % s, 5 if s else 7
+        for r in range(16):
+            mm(B[bk][:, 8:16], bw[:, 15 - r:143 - r], z(zs, r, 128, 16), r == 0, r == 15, [zk, bwk], bk)
+        join(16)
+        aff("mob", MO(s, 8, 16), vo, [vk], [m + "b"])
+        cp(IW["ui"], B[bk][:, 8:16], [], ["ui"], [bk])
+        ts(IW["v37"], vo, 37.0, -37.0, OP.mult, OP.add, [vk], ["v37"])
+        ts(IW["u12"], IW["ui"], 4095, None, OP.bitwise_and, None, ["ui"], ["u12"])
+        ts(IW["m5"], IW["ui"], 31, None, OP.bitwise_and, None, ["ui"], ["m5"])
+        tt(IW["sq"], IW["u12"], IW["u12"], OP.mult, ["u12"], ["sq"])
+        tt(MO(s, 16, 24), IW["m5"], T.j32[:], OP.add, ["m5", "j32"], [m + "c"])
+        ts(IW["q5"], IW["sq"], 5, None, OP.arith_shift_right, None, ["sq"], ["q5"])
+        tt(IW["s1"], IW["q5"], IW["v37"], OP.add, ["q5", "v37"], ["s1"])
+        ts(IW["vw"], IW["s1"], 1023, None, OP.bitwise_and, None, ["s1"], ["vw"])
+        ts(MO(s, 0, 8), IW["vw"], 1.0, None, OP.add, None, ["vw"], [m + "a"])
+        ks = [m + "a", m + "b", m + "c"]
+        if s == 0:
+            send(MO(s), [(nxt, ML(1), T.sem.al1)], ks, "m0")
+        elif s < NT - 1:
+            send(MO(s), [(nxt, MN(s), T.sem["an%d" % s]), (nx2, ML(s + 1), T.sem["al%d" % (s + 1)])], ks, "m%d" % s)
+        else:
+            send(MO(s), [(nxt, MN(s), T.sem["an%d" % s])], ks, "m%d" % s)
+
+    def lists(t):
+        cp(T.vl[:, 16 * t:16 * t + 16], ML(t, 0, 16), ["ml%d" % t], ["vl%d" % t])
+
+    def repeats(F, buf, fk, t, h, bk):
+        l, k, w = T.vl[:, 16 * t + 8 * h:16 * t + 8 * h + 8], "vl%d" % t, T.ft[:, 0:1025]
+        act(F(t, 8, 136), ind(w, l), AF.Copy, [k, "ft", "me"], [fk + "e%d" % t], scale=me)
+        act(F(t, 136, 264), ind(w, l), AF.Copy, [k, "ft", "mo"], [fk + "o%d" % t], scale=mo)
+        for gg in range(8):
+            c0 = 264 * t + (136 if gg % 2 else 8)
+            f = buf[32 * (gg // 2):32 * (gg // 2) + 32, c0:c0 + 128]
+            o = B[bk + gg // 4][:, 128 * (gg % 4):128 * (gg % 4) + 128]
+            mm(o, T.nbig[:, 0:128], T.u01[:], True, False, ["nbig", "u01"], bk + gg // 4)
+            mm(o, f, f, False, True, [fk + ("o%d" if gg % 2 else "e%d") % t], bk + gg // 4)
+            join(2)
+            if gg % 4 == 1:
+                ops[-1]["w"] = ["tile%d" % (gg // 4)]
+            if gg % 4 == 2:
+                ops[-1]["r"].append("tile%d" % (gg // 4))
+        for gg in range(8):
+            act(T.eq[:, :, gg, :], B[bk + gg // 4][:, 128 * (gg % 4):128 * (gg % 4) + 128], AF.Relu, [], ["eq%d" % gg], [bk + gg // 4], bias=-15.0)
+        for c in range(8):
+            mm(B[7][:, 8 + c:9 + c], T.eq[:, c, :, :], T.bigc[:, 0:1], True, True, ["eq%d" % i for i in range(8)] + ["bigc"], 7)
+        join(8)
+        aff("cnt", F(t, 0, 8), B[7][:, 8:16], [], [fk + "c%d" % t], [7])
+        if fk == "fo" and t < NT - 1:
+            send(F(t), [(nxt, FI(t + 1), T.sem["af%d" % (t + 1)])], ["foc%d" % t, "foe%d" % t, "foo%d" % t], "f%d" % t)
+
+    def targets(t):
+        mm(B[7][:, 16:32], T.iff[:], ML(t, 0, 16), True, False, ["iff", "ml%d" % t], 7, 4)
+        for h in range(2):
+            mm(B[7][:, 16 + 8 * h:24 + 8 * h], T.ib[:], FI(t, 0, 8), False, False, ["ib", "fic%d" % t], 7)
+            mm(B[7][:, 16 + 8 * h:24 + 8 * h], T.ib[:], FO(t, 0, 8), False, h == 1, ["ib", "foc%d" % t], 7)
+        join(5)
+        tt(T.om[:], B[7][:, 16:32], T.dump[:], OP.min, ["dumpa", "dumpb"], ["om"], [7])
+        cp(T.osc[:], T.om[:], ["om"], ["osc"])
+
+    def look(tab, k, off, ok, gbuf, gk, h, lv, rbuf, rk, c0, last):
+        a, m, e = 64 * h, 64 * h + lv, 64 * h + 64
+        w = tab[:, 0:1025]
+        act(gbuf[:, 16 * m:16 * e], ind(w, off[:, m:e]), AF.Identity, [k, k + "0", ok], [gk + "s"], bias=-2048.0)
+        ts(gbuf[:, 16 * a:16 * m], ind(w, off[:, a:m]), -2048.0, None, OP.add, None, [k, k + "0", ok], [gk + "v"])
+        o = B[h][:, c0:c0 + 64]
+        mm(o, T.nif[:], rbuf[:, 64 * h:64 * h + 64], True, False, ["nif", rk], h, 4)
+        if last:
+            mm(o, T.ones[:], T.c48[:], False, False, ["ones", "c48"], h)
+        for i in range(16):
+            mm(o, T.dk[:, 128 * i:128 * i + 128], gbuf[:, 1024 * h + i:1024 * h + 1024:16], False, i == 15, ["dk", gk + "v", gk + "s"], h)
+        join(16)
+
+    XK = ["xa", "xb", "xe", "xe2"]
+    xgk = ["xg0", "xg1", "xgs", "xg2", "xg3"]
+
+    def scat(tab, k, h):
+        tt(ind(tab[:, 0:1153], T.osc[:, 8 * h:8 * h + 8]), T.ep[:], T.rr[:, 128 * h:128 * h + 128], OP.max,
+           ["ep", "rr%d" % h, "osc"] + [k + str(i) for i in range(4)], [k])
+
+    def decode(when):
+        for i, (bk, wh) in enumerate(DEC):
+            if wh == when:
+                tab, k, out, ok = ((T.vd, "vd", T.ov, "ov"), (T.pd, "pd", T.op_, "op"))[i // 4]
+                a, o = tab[:, 1 + 256 * (i % 4):257 + 256 * (i % 4)], out[:, 1 + 256 * (i % 4):257 + 256 * (i % 4)]
+                act(B[bk][:, 0:256], a, AF.Relu, [k], ["pb%d" % bk], [bk], scale=0.5, bias=-2048.0)
+                tt(o, a, B[bk][:, 0:256], OP.subtract, [k, "pb%d" % bk], [ok + str(i % 4)], [bk])
+
+    lists(0)
+    chain(0)
+    repeats(FI, T.fi, "fi", 0, 1, 2)
+    repeats(FO, T.fo, "fo", 0, 0, 4)
+    for h in range(2):
+        encode(T.rv, T.vd, "vd", h, h)
+    for h in range(2):
+        encode(T.rp, T.pd, "pd", h, h)
+
+    for t in range(NT):
+        vl = T.vl[:, 16 * t:16 * t + 8]
+        sect[0] = ""
+        seen.clear()
+        ts(T.o1[:], ind(T.vd[:, 0:1025], vl), 4094.0, 0.5, OP.subtract, OP.mult, ["vd", "vd0", "vl%d" % t], ["o1"])
+        act(T.r1[:], ind(T.vd[:, 0:1025], vl), AF.Relu, ["vd", "vd0", "vl%d" % t], ["r1"], bias=4096.0, scale=-1.0)
+        for h in range(2):
+            look(T.pd, "pd", T.o1, "o1", T.g2, "g2%d" % h, h, LV[h], T.r1, "r1", 0, False)
+            ts(T.o2[:, 64 * h:64 * h + 64], B[h][:, 0:64], 2046.0, 0.5, OP.subtract, OP.mult, [], ["o2%d" % h], [h])
+            act(T.r2[:, 64 * h:64 * h + 64], B[h][:, 0:64], AF.Relu, [], ["r2%d" % h], [h], bias=2048.0, scale=-1.0)
+        for h in range(2):
+            look(T.vd, "vd", T.o2, "o2%d" % h, T.g3, "g3%d" % h, h, LV[2 + h], T.r2, "r2%d" % h, 64, True)
+            ts(T.o3[:, 64 * h:64 * h + 64], B[h][:, 64:128], -4096.0, None, OP.add, None, [], ["o3%d" % h], [h])
+        targets(t)
+        mm(B[6][:, 256:384], ZI(t), T.ib[:], True, True, ["z%d" % t, "ib"], 6)
+        aff("zt", T.zt[:], B[6][:, 256:384], [], ["zt"], [6])
+        if t == NT - 1:
+            decode(0)
+        act(T.xg[:, 16 * (64 - XS):1024], ind(T.xw[:], T.o3[:, 64 - XS:64]), AF.Copy, XK + ["o30"], ["xgs"])
+        for q in range(4):
+            a, e = 32 * q, (64 - XS if q == 1 else 32 * q + 32)
+            cp(T.xg[:, 16 * a:16 * e], ind(T.xw[:], T.o3[:, a:e]), XK + ["o3%d" % (q // 2)], ["xg%d" % q])
+            mm(B[2 + q][:], T.zt[:], T.ee[:, 512 * q:512 * q + 512], True, False, ["zt", "ee%d" % q], 2 + q)
+            mm(B[2 + q][:], T.ib[:], T.xg[:, 512 * q:512 * q + 512], False, True, ["ib", "xg%d" % q] + (["xgs"] if q == 1 else []), 2 + q)
+            act(T.ab[:, 512 * q:512 * q + 512], B[2 + q][:], AF.Abs, ["pb%d" % (2 + q)], ["ab%d" % q], [2 + q])
+        mm(B[6][:, 0:128], T.ib[:], T.kc[:], True, False, ["ib", "kc"], 6)
+        for k in range(16):
+            mm(B[6][:, k:128:16], T.ab[:, k:2048:16], T.b16[:], False, k == 15, ["ab0", "ab1", "ab2", "ab3", "b16"], 6)
+        join(16)
+        ts(T.ff[:], T.o3[:], 4096.0, 0.5, OP.is_lt, OP.max, ["o30", "o31"], ["ff"])
+        cp(T.nl[:], MN(t, 16, 24), [MNk[t][2]], ["nl"])
+        for h in range(2):
+            tt(T.e4[:, 64 * h:64 * h + 64], T.ff[:, 64 * h:64 * h + 64], B[h][:, 64:128], OP.mult, ["ff"], ["e4%d" % h], [h])
+        tt(T.nme[:], ind(T.iot[:], T.nl[:]), T.e4[:], OP.subtract, IOT + ["nl", "e40", "e41"], ["nme"])
+        aff("ev", B[5][:, 256:384], T.e4[:], ["e40", "e41"], ["ev", "pb5"], [5], bias=-4096.0)
+        if t < NT - 1:
+            ts(T.nx[:, 0:2], MN(t, 16, 18), 2.0, None, OP.mult, None, [MNk[t][2]], ["nx"])
+            lists(t + 1)
+            repeats(FO, T.fo, "fo", t + 1, 0, 2)
+        else:
+            decode(1)
+        op("V", lambda: V.tensor_tensor_scan(T.pm[:], T.rs[:], B[6][:, 0:128], 0.0, OP.add, OP.min), ["rs"], ["pmin"], [6], dur=128.0)
+        cp(T.key[:], B[6][:, 0:128], [], ["key"], [6])
+        tt(T.near[:], B[6][:, 0:128], T.tha[:], OP.is_lt, ["tha"], ["near"], [6])
+        tt(T.ge[:], ind(T.pm[:], T.bc[:]), T.key[:], OP.is_equal, ["pmin", "bc", "key"], ["ge"])
+        w2, plain = (T.w2[:, 0:128], 0.0) if t < NT - 1 else (T.w2[:, 128:256], 2048.0)
+        for h, F, fk, bk in ((0, FI, "fi", 1), (1, FO, "fo", 4)):
+            mm(B[bk][:, 0:128], w2, F(t, 8, 136), True, False, ["w2", fk + "e%d" % t], bk)
+            mm(B[bk][:, 0:128], w2, F(t, 136, 264), False, False, ["w2", fk + "o%d" % t], bk)
+            mm(B[bk][:, 0:128], T.near[:], T.nbig[:, 128 * h:128 * h + 128], False, True, ["near", "nbig", "pbig"], bk)
+            aff("rr%d" % h, T.rr[:, 128 * h:128 * h + 128], B[bk][:, 0:128], [], ["rr%d" % h], [bk], bias=plain - BIG * h)
+        mm(B[0][:, 128:256], T.ge[:], T.ib[:], True, True, ["ge", "ib"], 0)
+        tt(T.t1[:], B[0][:, 128:256], T.nme[:], OP.mult, ["nme"], ["t1"], [0])
+        tt(T.ep[:], T.t1[:], B[5][:, 256:384], OP.add, ["t1", "ev"], ["ep"], [5])
+        if t < NT - 1:
+            scat(T.vd, "vd", 0)
+            scat(T.pd, "pd", 1)
+        else:
+            scat(T.ov, "ov", 0)
+            scat(T.op_, "op", 1)
+        aff("oh", T.oh[:], B[0][:, 128:256], [], ["oh"], [0])
+        mm(B[5][:, 0:8], T.iff[:], T.j16[:], True, False, ["iff", "j16"], 5, 4)
+        for r in range(16):
+            mm(B[5][:, 0:8], T.bk[:, 15 - r:143 - r], T.oh[:, r:128:16], False, r == 15, ["bk", "oh"], 5)
+        join(16)
+        cp(T.kl[:], B[5][:, 0:8], [], ["kl"], [5])
+        tt(T.df[:], ind(T.xg[:], T.kl[:]), ZI(t), OP.subtract, xgk + ["kl", "z%d" % t], ["df"])
+        act(ZO(t), T.df[:], AF.Abs, ["df"], ["zo%d" % t])
+        aff("z192", T.z192[:], ZI(t), ["z%d" % t], ["z192"], bias=-192.0, f=0.5)
+        ts(T.tt[:], T.df[:], 0.5, 191.75, OP.mult, OP.add, ["df"], ["tt"], f=0.5)
+        tt(ind(T.xw[:, 0:4096], T.nl[:]), T.tt[:], T.z192[:], OP.add, ["tt", "z192", "nl"], ["xa", "xb"])
+        if t < NT - 1:
+            tt(ind(T.xw[:, 4096:6144], T.nx[:, 0:2]), T.tt[:, 0:32], T.z192[:, 0:32], OP.add, ["tt", "z192", "nx"], ["xe2"])
+            send(ZO(t), [(nxt, ZI(t + 1), T.sem["az%d" % (t + 1)])], ["zo%d" % t], "z%d" % t)
+            chain(t + 1)
+            mm(B[6][:, 128:256], T.ones[:], T.near[:], True, True, ["ones", "near"], 6)
+            act(T.g128[:], B[6][:, 128:256], AF.Identity, [], ["ac0", "g128"], [6], scale=-16.0, acc=T.ac[:, 0:1])
+            aff("aq", T.aq[:, 0:1], T.ac[:, 0:1], ["ac0"], ["aq"], scale=1.0 / 4096.0, bias=192.502)
+            aff("ac", T.ac[:, 1:2], T.aq[:, 0:1], ["aq", "ac0"], ["ac1"], scale=-4096.0, bias=T.ac[:, 0:1])
+            aff("tha", T.tha[:], T.th16[:], ["th16", "ac1"], ["tha"], bias=T.ac[:, 1:2])
+
+    t = NT - 1
+    sect[0] = "e"
+    dma("Y", T.yz[:], ZO(t), ["zo%d" % t], [], 32)
+    dma("Y", T.yvd[:], T.ov[:, 1:1025], ["ov"], [], 512)
+    dma("Y", T.ypd[:], T.op_[:, 1:1025], ["op"], [], 512)
+    for h, bk in ((0, 1), (1, 4)):
+        for i in range(4):
+            l = T.ib[:] if i == 0 else T.sc3[:, 128 * i - 128:128 * i]
+            mm(B[bk][:], l, T.xw[:, 1024 * i + 512 * h:1024 * i + 512 * h + 512], i == 0, i == 3, ["ib", "sc3", "xa", "xb"], bk)
+        act(T.ox[:, 512 * h:512 * h + 512], B[bk][:], AF.Copy, [], ["ox%d" % h], [bk])
+        dma("Y", T.yx[:, 512 * h:512 * h + 512], T.ox[:, 512 * h:512 * h + 512], ["ox%d" % h], [], 256)
+    cp(T.yl[:], MN(t, 0, 16), [MNk[t][0]], ["yl"])
+    ts(T.ya[:], ind(T.iot[:, 0:1536], T.yl[:, 8:16]), 1024.0, -4097.0 * 1025.0, OP.mult, OP.add, ["yl"] + IOT[:3], ["ya"])
+    tt(T.yb[:], ind(T.iot[:, 0:1536], T.yl[:, 0:8]), T.ya[:], OP.add, ["yl", "ya"] + IOT[:3], ["yb"])
+    dma("Y", T.yvp[:], T.yb[0:128:16, :], ["yb"], [])
+    emit(g, T, arrange(ops))

@@ -5,10 +5,15 @@ F32, BF, F16, I32, U16 = "float32", "bfloat16", "float16", "int32", "uint16"
 NT = 4
 BIG = 8192.0
 LV = (24, 24, 24, 24)
-XS = 24
-ONV = ("mob", "cnt", "zt", "ev", "z192", "aq", "ac", "tha")
+XS = 20
+DQ = ((0, 2), (2, 3), (3, 4))
+NI = (1, 2, 3)
+LM = (1, 1)
+ONV = ("ev", "z192")
 DEC = ((2, 1), (3, 1), (2, 1), (3, 1), (4, 0), (5, 0), (4, 0), (5, 0))
-GAT, SCA, HOP, FAR = 1.56, 3.5, 70.0, 2000.0
+KBT = 5.0
+PEC = 0.55
+GAT, SCA, HOP, FAR = 1.56, 3.5, 100.0, 2200.0
 
 
 def _sb(n, d):
@@ -22,16 +27,17 @@ SCRATCH = {
     "thf": _sb(128, F32), "th16": _sb(128, F32), "tha": _sb(128, F32),
     "ci": _sb(16, I32), "cf": _sb(16, F32), "l16": _sb(16, F32), "m16": _sb(16, F32), "sg": _sb(16, F32),
     "pw": _sb(16, F32), "pw2": _sb(16, F32), "two": _sb(16, F32), "c16": _sb(8, F32), "jj": _sb(8, F32),
-    "j32": _sb(8, F32), "j16": _sb(8, F32), "dump": _sb(16, F32), "bci": _sb(8, I32), "bc": _sb(8, U16),
-    "x144": _sb(144, F32), "g128": _sb(128, F32), "bs": _sb(144, BF), "bw0": _sb(144, BF), "bw1": _sb(144, BF),
-    "bk": _sb(144, BF), "blk": _sb(128, BF), "b16": _sb(8, BF), "kc": _sb(128, BF),
+    "j32": _sb(8, F32), "j16": _sb(8, BF), "dump": _sb(16, F32), "bci": _sb(8, I32), "bc": _sb(8, U16),
+    "g128": _sb(128, F32), "bw0": _sb(128, BF), "bw1": _sb(128, BF), "mr": _sb(128, BF), "sel": _sb(8, F32),
+    "um": _sb(128, F32), "km": _sb(128, BF), "bk": _sb(128, BF), "blk": _sb(128, BF), "b16": _sb(8, BF), "kc": _sb(128, BF),
     "rs": _sb(128, F32), "ones": _sb(128, BF), "onef": _sb(128, F32), "ib": _sb(128, BF),
-    "iff": _sb(128, F32), "nif": _sb(128, F32), "nbig": _sb(256, BF), "sc3": _sb(384, BF), "u01": _sb(128, BF),
+    "iff": _sb(128, F32), "nif": _sb(128, F16), "nbig": _sb(256, BF), "sc3": _sb(384, BF),
     "c48": _sb(64, BF), "bigc": _sb(8, BF), "w2": _sb(256, BF), "dk": _sb(2048, F16), "ee": _sb(2048, BF),
     "ft": _sb(1040, BF), "iot": _sb(4096, F32),
-    "eq": ("sbuf", [128, 8, 8, 16], BF), "vl": _sb(64, U16),
+    "eq": ("sbuf", [128, 8, 8, 16], BF), "vl": _sb(64, U16), "er": _sb(1024, BF), "fu": _sb(128, BF),
+    "x144": _sb(144, F32), "bs": _sb(144, BF), "sw0": _sb(144, BF), "sw1": _sb(144, BF), "sk": _sb(144, BF),
     "om": _sb(16, F32), "osc": _sb(16, U16), "nl": _sb(8, U16), "nx": _sb(8, U16),
-    "o1": _sb(128, U16), "o2": _sb(128, U16), "o3": _sb(128, U16), "r1": _sb(128, F32), "r2": _sb(128, F32),
+    "o1": _sb(128, U16), "o2": _sb(128, U16), "o3": _sb(128, U16), "r1": _sb(128, F16), "r2": _sb(128, F16),
     "g2": _sb(2048, F16), "g3": _sb(2048, F16), "xg": _sb(2048, BF), "ab": _sb(2048, BF), "zt": _sb(128, BF),
     "ff": _sb(128, F32), "e4": _sb(128, F32), "nme": _sb(128, F32), "pm": _sb(128, F32),
     "near": _sb(128, BF), "ge": _sb(128, BF), "key": _sb(128, F32), "t1": _sb(128, F32), "ep": _sb(128, F32), "rr": _sb(256, F32),
@@ -50,8 +56,11 @@ SEMAPHORES = (["cV", "cS", "cP", "cG", "sent", "aw"] + ["d%d" % i for i in range
 
 PUSH = {x.split(":")[0]: 100 * int(x.split(":")[1]) for x in """
 sYvni.1:900 sYrv0.1:800 sYrv1.1:700 sYrp0.1:600 sYrp1.1:500 sYxa.1:400 sSpni.1:900 sSwi.1:800 sSz.1:700 sSthi.1:600
-Vzt6.1:140 Vxg1.1:336 Pfoe2.2:-297 Seq02.1:-268 Vov13.1:-189 Sr200.1:96 Pzt5.1:-193 Vov22.1:-120 Vov.1:22 Vsq.1:169 Vu12.1:122 Szo.1:261 sVblk.1:-34 Vvl.1:184 sGg128.1:105 sVxe.4:-24 sVs1.1:-16 sPfoe4.2:-326 Spb33.1:-65 sVtwo.1:-32 sVci2.1:6 Vvw.1:129 sVsq.1:116 Pnear4.1:34 sSiff.1:-209 sSeq55.1:-113 Seq22.1:61 sGiot7.1:-87 sVdk.6:-80 Vop24.1:11 Soh0.1:-20 Vnl.1:50 sVbs.1:41 sVdk.11:-52 sGl16.1:38 Vff.1:-41 sGci0.1:162 sGkc.1:-54 sGiot5.1:-35 Vmob.1:74 Vxg0.1:27 Vz92.1:-93 sSdumpa.1:-97 sSbk.1:-153 eVya.1:90 Vs1.1:115 Vkl5.1:-16 Seq63.1:-126 Vui5.1:38 sPfie3.2:-58 sVxe.2:-15 sVj32.1:60 Vo300.1:-5 Sxgs.1:59 sGee3.1:-56 Pnif1.2:-62 sVmoc.1:115 Vmoc.1:53 Pib4.1:-125 sVwc.1:-56 sVjj.1:-9 Sg21s.1:130 Seq53.1:46 Pnif0.2:-129 Seq12.1:59 Seq32.1:34 Vxe2.1:18 sSth166.1:-76 sSeq43.1:-70 sVmo.1:165 sVme.1:78 sSft.10:-185 sVfic7.1:-7 Vov02.1:-185 Vo200.1:-17 sSfio.1:87 Vnx.1:-73 sVdk.7:24 sGiot4.1:-92 Pbw15.1:-121 Sr1.1:-89 sGiot0.1:-18 sVm.1:-5 Pbigc7.1:-12 sVm6.1:65 sVpd0.1:-49 sVgb.1:60 sPfoe4.4:38 Vg30v.1:18 sVee2.1:-7 ePib4.1:-15 sVdk.10:-52 Vnme.1:51 sVpd0.2:-42 Vtt.1:-90 sVenc11.2:-19 Spb44.2:15 sGbci.1:-50 Pw24.2:-68 sVdk.15:-20 sSnif.1:-30 Vpmin6.1:-24 Pfoo3.2:45 Srr14.1:75 sVee0.1:-10 sSeq02.1:-20 Sab24.1:5 Pzt4.1:40 Vg20v.1:-10 Vom7.1:25 sPbigc7.2:40 Vg31v.1:40
+Vee.5:-79 Vq5.1:-48 sVpw.1:-35 Vnl.1:-146 Vnx.1:-43 Vv37.1:-89 Vmoc.1:-63 sVpwa.1:-68 sVci1.1:-61 Pfoo3.2:221 sVxe.2:-55 eVya.1:-40 Ve411.1:112 sVjj.1:-34 Vvd.1:-45 Vz92.1:-290 Pw21.2:-56 Stt.1:32 sSiff.1:-200 Pab06.17:62 Vui5.1:-66 Vnear6.1:152 sVw0.1:-7 sSfic7.1:202 Vop35.1:85 Vff.1:-54 sSdumpa.1:-87 sVblk.1:45 Vev5.1:21 Saq.1:-65 sVv37.1:26 Spb22.2:-52 sVrs.1:-41 Soh0.1:-47 Vee.10:38 sVenc11.2:-52 Vg31v.1:-51 eVyl.1:50 Sab1.1:97 Vxg2.1:63 sGiot4.1:38 sVsel.1:180 sVpwb.1:-105 Vee.14:-45 sVones.1:-46 Vo311.1:-62 Pfoo2.1:-60 Pw24.1:-45 sVbk.1:95 sVs1.1:-28 Vov13.1:-70 Vo1.1:64 Vg21v.1:137 Vum5.1:33 Szo.1:42 Seq32.1:-22 sVdk.8:19 sGkc.1:22 sVnif.1:-44 Vo300.1:50 Sg21s.1:35 Seq63.1:-24 Vnme.1:27 Vsq.1:-36 Seq02.1:12 sPonef6.1:-30 sVpwc.1:-70 Vom7.1:-85 Vo211.1:-47 ePib1.1:-30 Pfoo3.1:-8 Spb55.1:-30 Vee.9:-5 sSeq02.1:-42 sGl16.1:5 sVvd0.1:-40 sPfie2.1:-2
 """.split()}
+
+
+ORDER = "0=0>0H0J0?0B1H0@310I0A1J0M2R231D1G1F1L0K1I1E1O271N0L1K380C282A103611122B2C261A2D1M291P2E1Q2F2G1R132:1S240D141T252H1U2I2J2<1V150O2=161W1C172K2?39373:18203D4W0E3;213E2L500V4A19513F3R0F3S3T3340524@3<0P3U3=2M3V2N3W3G3>0G534B41444F4C5T421:430N544D4E454G0U1;550R3I575U2O560S0W5W4H4I2P1@595:2@585?1B465;5<1<5@4:5A485=1=5B3H5E5F4900473J5>5C5D5G5H3K1>5M5K5N4=1?5I3M3L5L4<613N4;5J3O4J64650T605O5V4>4K5P3P68623Q66634P696<676=4N6:4R2Q2W6>6;226C4S2U6F6@042V6E2S3?6?4L2;3@2T80306A2>4O6J3A4?326K6D6B34354Q6L7B7:6Q0Q7>7;4M6R7<7C7?7=7D7@4T6H7A6G6S6I4U7F7E4V5Q7G7P7K7H6T5R6M6V6N5S8:7I6O6P7L8;757J6U768?7M8@8A6W027N8C8I748B717O7Q8H8D8G7T7U728E7R8M708F8J8N737W8O8P8K81017S8S8Q8L8T8U8V77838R859894788W95797V96999082868<9<9=8=8>87849:889@89979;9A9>069D9E9?9B919C9F923B03089K;09H9N9G939R9M9Q3C9L;89O9S9I9P9T9J:1:B:2:C:3:4:E:F:6:J:K:D9U:N:L:O9V:G:M9W:P:;;B:S:H:R:0:I:T:=:5:Q:<;C:U:::V;G:W;1;H;I;4;5;J:>;K;P:7;O;L:9;7;2;Q:805;M;:;R;9;U;3;V<<:?;N;S;T;W<=;;<0<4<1<3;=<I<2;<;><@<5<?<A;D;6:@<><6<7;?<D;E;F<B<8;@<H;A<E<C<F:A<9<L<G<J<M<K>7<:<N<;<S070<<U<P<V<O<T=1=2<W0:=3<Q=0>==4<R=9=I=Q=5=J=R=K=M=N=L=S>I>J=U=6=V=T=7=:=W>2=O>?=;>1=P=<>3=>>0?E=F>4>N=D>5>P?F=E>8>O>Q>R=8>6?I>;><>W>V=C>S>9>>==?0?1>T>@?5?4=@09?C>U>B>A?6=B>D>C?2?3?J?<?7?==?>:?G?8?;=A?D?:?T>E?9?H?P>F?S=G?O?M?>?K?U=H??>G?W>H?Q?V@0?R?N?L@1@3?@@B@4@2@:@50;@=@<@;AH@7@C@6A6?A@>>K@8@?>L>M@9@@@P@H@F@L@Q@I@M@J@K@R@S?B@T@N@UA1@VA0A2@AA;@DA3A4@O@EA5@GA7@WA8AIA9A<A:AJABA=A>A?ACA@ADAEAAAFAGAK"
 
 
 def planner(ops):
@@ -140,11 +149,14 @@ def planner(ops):
         return span, order, after
 
     tail = tails(plan([0.0] * n)[1], {})
-    return lambda push: plan([x + push.get(o["cls"], 0) for x, o in zip(tail, ops)])
+    return (lambda push: plan([x + push.get(o["cls"], 0) for x, o in zip(tail, ops)])), pre
 
 
 def arrange(ops):
-    order = planner(ops)(PUSH)[1]
+    if ORDER:
+        order = [40 * (ord(ORDER[i]) - 48) + ord(ORDER[i + 1]) - 48 for i in range(0, len(ORDER), 2)]
+    else:
+        order = planner(ops)[0](PUSH)[1]
     return [ops[i] for i in order if ops[i]["kind"] == "a"] + [ops[i] for i in order if ops[i]["kind"] != "a"]
 
 
@@ -290,7 +302,7 @@ def rank_program(g, core, T, topo):
             act(out, a, AF.Identity, r, w, b, bias=bias, scale=scale)
 
     def mm(out, l, rh, st, sp, r, bk, f=1.0):
-        op("P", lambda: P.matmul(out, l, rh, st, sp), r, (), [bk], dur=10.0 + 0.5 * f * max(min(64, els(l)), els(rh)))
+        op("P", lambda: P.matmul(out, l, rh, st, sp), r, (), [bk], dur=PEC * f * max(min(64, els(l)), els(rh)))
 
     def join(k):
         part_ = ops[-k:]
@@ -309,7 +321,7 @@ def rank_program(g, core, T, topo):
 
     def dma(q, out, a, r, w, kb=0):
         e = {"Y": g.sync, "S": S, "G": g}[q]
-        op(q, lambda: e.dma_start(out, a), r, w, kind="d", dur=60.0 + 4.0 * kb, lat=2000.0)
+        op(q, lambda: e.dma_start(out, a), r, w, kind="d", dur=60.0 + KBT * kb, lat={"z0": 3500.0, "thi": 4700.0}.get((list(w) + [0])[0], 2100.0))
 
     def eng(a, c):
         return len(topo.engines(a, c))
@@ -372,23 +384,21 @@ def rank_program(g, core, T, topo):
     iota(T.l16[:], [[1, 16]], 0, 0, ["l16"])
     asel(T.ib[:], T.ones[:], [[-1, 128]], OP.is_equal, 0, 1, ["ones"], ["ib"])
     iota(T.c16[:], [[16, 8]], 0, 0, ["c16"])
-    iota(T.x144[:], [[1, 144]], -15, 0, ["x144"])
     iota(T.g128[:], [[16, 8], [0, 16]], 0, 0, ["g128"])
-    asel(T.u01[:], T.ones[:], [[-1, 128]], OP.is_ge, 0, 1, ["ones"], ["u01"])
     iota(T.kc[:], [[0, 8], [1, 16]], 0, 0, ["kc"])
     iota(T.bci[:], [[16, 8]], 15, 0, ["bci"], False)
     IOT = ["iot%d" % i for i in range(8)]
     for i in range(8):
-        if i in (1, 2):
+        if i in NI:
             act(T.iot[:, 512 * i:512 * i + 512], T.iot[:, 0:512], AF.Identity, ["iot0"], [IOT[i]], bias=512.0 * i)
         else:
             iota(T.iot[:, 512 * i:512 * i + 512], [[1, 512]], 4096 + 512 * i, 0, [IOT[i]])
     for q in range(4):
-        ms(T.ee[:, 512 * q:512 * q + 512], -1.0, ["ee%d" % q])
-        asel(T.ee[:, 512 * q:512 * q + 512], T.ee[:, 512 * q:512 * q + 512], [[-1, 32], [0, 16]], OP.is_equal, -32 * q, 1, ["ee%d" % q], ["ee%d" % q])
-        ms(T.xw[:, 4096 + 512 * q:4608 + 512 * q], 0.0, ["xe"])
+        for k in range(4 * q, 4 * q + 4):
+            ts(T.ee[:, k:2048:16], T.ib[:], -1.0, None, OP.mult, None, ["ib"], ["ee"], f=0.5)
     for q in range(2):
-        cp(T.xw[:, 4096 + 1024 * q:5120 + 1024 * q:2], T.xw[:, 512 * q:512 * q + 512], ["xa", "xe"], ["xe2"], f=0.5)
+        cp(T.xw[:, 4096 + 1024 * q:5120 + 1024 * q:2], T.xw[:, 512 * q:512 * q + 512], ["xa"], ["xe2"], f=0.5)
+        iota(T.xw[:, 4097 + 1024 * q:5120 + 1024 * q:2], [[0, 512]], 0, 0, ["xe"])
     ms(T.ft[:, 0:2], -1.0, ["ft"])
     ms(T.two[:], 2.0, ["two"])
     ts(T.ci[:, 1:2], T.ci[:, 0:1], 15, None, OP.bitwise_and, None, ["ci0"], ["ci1"])
@@ -408,16 +418,31 @@ def rank_program(g, core, T, topo):
     ts(ML(0, 0, 8), T.vni[:], 1.0, None, OP.add, None, ["vni"], ["ml0"])
     ts(ML(0, 8, 16), T.pni[:], 1.0, None, OP.add, None, ["pni"], ["ml0"])
     ts(T.jj[:], T.c16[:], pm, None, OP.add, None, ["c16", "pm_"], ["jj"])
-    ts(T.bs[:], T.x144[:], gb, None, OP.is_equal, None, ["x144", "gb"], ["bs"])
+    ts(T.blk[:], T.g128[:], gb, None, OP.is_equal, None, ["g128", "gb"], ["blk"])
+    if 0 in LM:
+        ts(T.mr[:], T.kc[:], pm, None, OP.is_equal, None, ["kc", "pm_"], ["mr"], f=0.5)
+    if 1 in LM:
+        iota(T.x144[:], [[1, 144]], -15, 0, ["x144"])
+        ts(T.bs[:], T.x144[:], gb, None, OP.is_equal, None, ["x144", "gb"], ["bs"])
     cp(w0, T.wi[:, 0:1], ["wi"], ["w0"])
+    cp(w1, T.wn[:, 0:1], ["wn"], ["w1"])
     ts(T.j32[:], T.jj[:], 32.0, None, OP.mult, None, ["jj"], ["j32"])
-    ts(T.bw0[:], T.bs[:], w0, None, OP.mult, None, ["bs", "w0"], ["bw0"], f=0.5)
+    if LM[0]:
+        ts(T.sw0[:], T.bs[:], w0, None, OP.mult, None, ["bs", "w0"], ["bw0"], f=0.5)
+        ts(T.sw1[:], T.bs[:], w1, None, OP.mult, None, ["bs", "w1"], ["bw1"], f=0.5)
+    else:
+        cp(T.sel[:], T.blk[:, 0:128:16], ["blk"], ["sel"])
+        ts(T.bw0[:], T.blk[:], w0, None, OP.mult, None, ["blk", "w0"], ["bw0"], f=0.5)
+        ts(T.bw1[:], T.blk[:], w1, None, OP.mult, None, ["blk", "w1"], ["bw1"], f=0.5)
+    if LM[1]:
+        ts(T.sk[:], T.bs[:], pm, None, OP.mult, None, ["bs", "pm_"], ["bk"], f=0.5)
+    else:
+        ts(T.bk[:], T.blk[:], pm, 0.0625, OP.mult, OP.mult, ["blk", "pm_"], ["bk"], f=0.5)
     send(T.wi[:, 0:1], [(prv, T.wn[:, 0:1], T.sem.aw)], ["wi"], "w")
     for k in range(16):
         ts(T.dk[:, 128 * k:128 * k + 128], T.ib[:], T.m16[:, k:k + 1], None, OP.mult, None, ["ib", "m16"], ["dk"], f=0.5)
-    ts(T.blk[:], T.g128[:], gb, None, OP.is_equal, None, ["g128", "gb"], ["blk"])
     op("V", lambda: V.tensor_tensor_scan(T.pw[:], T.two[:], T.ones[:, 0:16], 0.5, OP.mult, OP.mult), ["two", "ones"], ["pw"])
-    ms(T.c48[:], 48.0, ["c48"])
+    ms(T.c48[:], 32.0, ["c48"])
     ms(T.pw[:, 10:11], -4096.0, ["pwa"], ["pw"])
     ms(T.pw[:, 11:12], -1024.0, ["pwb"], ["pw"])
     ms(T.pw[:, 12:13], 1.0, ["pwc"], ["pw"])
@@ -430,10 +455,9 @@ def rank_program(g, core, T, topo):
     ts(T.w2[:, 0:128], T.blk[:], wc, None, OP.mult, None, ["blk", "wc"], ["w2"], f=0.5)
     ts(T.w2[:, 128:256], T.blk[:], wc, 0.5, OP.mult, OP.mult, ["blk", "wc"], ["w2"], f=0.5)
     act(T.nbig[:, 128:256], T.ib[:], AF.Copy, ["ib"], ["pbig"], scale=BIG)
-    act(T.nif[:], T.ib[:], AF.Copy, ["ib"], ["nif"], scale=-1.0)
+    cp(T.nif[:], T.ib[:], ["ib"], ["nif"], f=0.5)
     act(T.iff[:], T.ib[:], AF.Copy, ["ib"], ["iff"])
     act(T.j16[:], T.jj[:], AF.Copy, ["jj"], ["j16"], scale=16.0)
-    act(T.bk[:], T.bs[:], AF.Copy, ["bs", "pm_"], ["bk"], scale=pm)
     act(T.dump[:, 0:8], T.jj[:], AF.Identity, ["jj"], ["dumpa"], bias=1025.0)
     act(T.dump[:, 8:16], T.jj[:], AF.Identity, ["jj"], ["dumpb"], bias=1025.0)
     mm(B[6][:, 0:128], T.onef[0:1, :], T.thf[0:1, :], True, True, ["onef", "thf"], 6, 4)
@@ -441,8 +465,6 @@ def rank_program(g, core, T, topo):
     act(T.th16[:], B[6][:, 0:128], AF.Identity, [], ["th16"], [6], bias=790528.0)
     ts(T.rs[:], T.kc[:], 0.0, 65536.0, OP.is_equal, OP.mult, ["kc"], ["rs"])
     cp(T.bc[:], T.bci[:], ["bci"], ["bc"])
-    cp(w1, T.wn[:, 0:1], ["wn"], ["w1"])
-    ts(T.bw1[:], T.bs[:], w1, None, OP.mult, None, ["bs", "w1"], ["bw1"], f=0.5)
     for i, s in enumerate((64.0, 4096.0, 262144.0)):
         ts(T.sc3[:, 128 * i:128 * i + 128], T.ib[:], s, None, OP.mult, None, ["ib"], ["sc3"], f=0.5)
 
@@ -457,9 +479,15 @@ def rank_program(g, core, T, topo):
         bw, bwk = (T.bw0, "bw0") if s == 0 else (T.bw1, "bw1")
         vo, vk = (ML(0, 0, 8), "ml0") if s == 0 else (MN(s - 1, 0, 8), MNk[s - 1][0])
         m, bk = "mo%d" % s, 5 if s else 7
-        for r in range(16):
-            mm(B[bk][:, 8:16], bw[:, 15 - r:143 - r], z(zs, r, 128, 16), r == 0, r == 15, [zk, bwk], bk)
-        join(16)
+        if LM[0]:
+            sw = T.sw1 if s else T.sw0
+            for r in range(16):
+                mm(B[bk][:, 8:16], sw[:, 15 - r:143 - r], z(zs, r, 128, 16), r == 0, r == 15, [zk, bwk], bk)
+            join(16)
+        else:
+            mm(B[bk][:, 128:256], z(zs), bw[:], True, True, [zk, bwk], bk)
+            tt(T.um[:], B[bk][:, 128:256], T.mr[:], OP.mult, ["mr"], ["um"], [bk])
+            mm(B[bk][:, 8:16], T.um[:], T.sel[:], True, True, ["um", "sel"], bk, 4)
         aff("mob", MO(s, 8, 16), vo, [vk], [m + "b"])
         cp(IW["ui"], B[bk][:, 8:16], [], ["ui"], [bk])
         ts(IW["v37"], vo, 37.0, -37.0, OP.mult, OP.add, [vk], ["v37"])
@@ -484,21 +512,26 @@ def rank_program(g, core, T, topo):
 
     def repeats(F, buf, fk, t, h, bk):
         l, k, w = T.vl[:, 16 * t + 8 * h:16 * t + 8 * h + 8], "vl%d" % t, T.ft[:, 0:1025]
-        act(F(t, 8, 136), ind(w, l), AF.Copy, [k, "ft", "me"], [fk + "e%d" % t], scale=me)
-        act(F(t, 136, 264), ind(w, l), AF.Copy, [k, "ft", "mo"], [fk + "o%d" % t], scale=mo)
+        if "fu" in ONV:
+            act(T.fu[:], ind(w, l), AF.Copy, [k, "ft"], ["fu"])
+            ts(F(t, 8, 136), T.fu[:], me, None, OP.mult, None, ["fu", "me"], [fk + "e%d" % t], f=0.5)
+            ts(F(t, 136, 264), T.fu[:], mo, None, OP.mult, None, ["fu", "mo"], [fk + "o%d" % t], f=0.5)
+        else:
+            act(F(t, 8, 136), ind(w, l), AF.Copy, [k, "ft", "me"], [fk + "e%d" % t], scale=me)
+            act(F(t, 136, 264), ind(w, l), AF.Copy, [k, "ft", "mo"], [fk + "o%d" % t], scale=mo)
         for gg in range(8):
             c0 = 264 * t + (136 if gg % 2 else 8)
             f = buf[32 * (gg // 2):32 * (gg // 2) + 32, c0:c0 + 128]
             o = B[bk + gg // 4][:, 128 * (gg % 4):128 * (gg % 4) + 128]
-            mm(o, T.nbig[:, 0:128], T.u01[:], True, False, ["nbig", "u01"], bk + gg // 4)
-            mm(o, f, f, False, True, [fk + ("o%d" if gg % 2 else "e%d") % t], bk + gg // 4)
-            join(2)
+            mm(o, f, f, True, True, [fk + ("o%d" if gg % 2 else "e%d") % t], bk + gg // 4)
             if gg % 4 == 1:
                 ops[-1]["w"] = ["tile%d" % (gg // 4)]
             if gg % 4 == 2:
                 ops[-1]["r"].append("tile%d" % (gg // 4))
+        for q in range(2):
+            act(T.er[:, 512 * q:512 * q + 512], B[bk + q][:], AF.Relu, [], ["er%d" % q], [bk + q], bias=-15.0)
         for gg in range(8):
-            act(T.eq[:, :, gg, :], B[bk + gg // 4][:, 128 * (gg % 4):128 * (gg % 4) + 128], AF.Relu, [], ["eq%d" % gg], [bk + gg // 4], bias=-15.0)
+            asel(T.eq[:, :, gg, :], T.er[:, 128 * gg:128 * gg + 128], [[1, 128]], OP.is_gt, 0, -1, ["er%d" % (gg // 4)], ["eq%d" % gg])
         for c in range(8):
             mm(B[7][:, 8 + c:9 + c], T.eq[:, c, :, :], T.bigc[:, 0:1], True, True, ["eq%d" % i for i in range(8)] + ["bigc"], 7)
         join(8)
@@ -521,7 +554,7 @@ def rank_program(g, core, T, topo):
         act(gbuf[:, 16 * m:16 * e], ind(w, off[:, m:e]), AF.Identity, [k, k + "0", ok], [gk + "s"], bias=-2048.0)
         ts(gbuf[:, 16 * a:16 * m], ind(w, off[:, a:m]), -2048.0, None, OP.add, None, [k, k + "0", ok], [gk + "v"])
         o = B[h][:, c0:c0 + 64]
-        mm(o, T.nif[:], rbuf[:, 64 * h:64 * h + 64], True, False, ["nif", rk], h, 4)
+        mm(o, T.nif[:], rbuf[:, 64 * h:64 * h + 64], True, False, ["nif", rk], h)
         if last:
             mm(o, T.ones[:], T.c48[:], False, False, ["ones", "c48"], h)
         for i in range(16):
@@ -557,11 +590,11 @@ def rank_program(g, core, T, topo):
         sect[0] = ""
         seen.clear()
         ts(T.o1[:], ind(T.vd[:, 0:1025], vl), 4094.0, 0.5, OP.subtract, OP.mult, ["vd", "vd0", "vl%d" % t], ["o1"])
-        act(T.r1[:], ind(T.vd[:, 0:1025], vl), AF.Relu, ["vd", "vd0", "vl%d" % t], ["r1"], bias=4096.0, scale=-1.0)
+        ts(T.r1[:], ind(T.vd[:, 0:1025], vl), 4096.0, 2048.0, OP.min, OP.subtract, ["vd", "vd0", "vl%d" % t], ["r1"])
         for h in range(2):
             look(T.pd, "pd", T.o1, "o1", T.g2, "g2%d" % h, h, LV[h], T.r1, "r1", 0, False)
-            ts(T.o2[:, 64 * h:64 * h + 64], B[h][:, 0:64], 2046.0, 0.5, OP.subtract, OP.mult, [], ["o2%d" % h], [h])
-            act(T.r2[:, 64 * h:64 * h + 64], B[h][:, 0:64], AF.Relu, [], ["r2%d" % h], [h], bias=2048.0, scale=-1.0)
+            ts(T.o2[:, 64 * h:64 * h + 64], B[h][:, 0:64], 4094.0, 0.5, OP.subtract, OP.mult, [], ["o2%d" % h], [h])
+            ts(T.r2[:, 64 * h:64 * h + 64], B[h][:, 0:64], 4096.0, 2048.0, OP.min, OP.subtract, [], ["r2%d" % h], [h])
         for h in range(2):
             look(T.vd, "vd", T.o2, "o2%d" % h, T.g3, "g3%d" % h, h, LV[2 + h], T.r2, "r2%d" % h, 64, True)
             ts(T.o3[:, 64 * h:64 * h + 64], B[h][:, 64:128], -4096.0, None, OP.add, None, [], ["o3%d" % h], [h])
@@ -571,16 +604,20 @@ def rank_program(g, core, T, topo):
         if t == NT - 1:
             decode(0)
         act(T.xg[:, 16 * (64 - XS):1024], ind(T.xw[:], T.o3[:, 64 - XS:64]), AF.Copy, XK + ["o30"], ["xgs"])
+        mm(B[6][0:32 * DQ[0][1], 0:128], T.ib[:, 0:32 * DQ[0][1]], T.kc[:], True, False, ["ib", "kc"], 6)
         for q in range(4):
             a, e = 32 * q, (64 - XS if q == 1 else 32 * q + 32)
             cp(T.xg[:, 16 * a:16 * e], ind(T.xw[:], T.o3[:, a:e]), XK + ["o3%d" % (q // 2)], ["xg%d" % q])
-            mm(B[2 + q][:], T.zt[:], T.ee[:, 512 * q:512 * q + 512], True, False, ["zt", "ee%d" % q], 2 + q)
+            mm(B[2 + q][:], T.zt[:], T.ee[:, 512 * q:512 * q + 512], True, False, ["zt", "ee"], 2 + q)
             mm(B[2 + q][:], T.ib[:], T.xg[:, 512 * q:512 * q + 512], False, True, ["ib", "xg%d" % q] + (["xgs"] if q == 1 else []), 2 + q)
             act(T.ab[:, 512 * q:512 * q + 512], B[2 + q][:], AF.Abs, ["pb%d" % (2 + q)], ["ab%d" % q], [2 + q])
-        mm(B[6][:, 0:128], T.ib[:], T.kc[:], True, False, ["ib", "kc"], 6)
-        for k in range(16):
-            mm(B[6][:, k:128:16], T.ab[:, k:2048:16], T.b16[:], False, k == 15, ["ab0", "ab1", "ab2", "ab3", "b16"], 6)
-        join(16)
+        for a, e in DQ:
+            if a:
+                mm(B[6][32 * a:32 * e, 0:128], T.ib[:, 32 * a:32 * e], T.kc[:], True, False, ["ib", "kc"], 6)
+            for k in range(16):
+                mm(B[6][32 * a:32 * e, k:128:16], T.ab[:, 512 * a + k:512 * e:16], T.b16[:], False, k == 15,
+                   ["ab%d" % q for q in range(a, e)] + ["b16"], 6)
+            join(17 if a else 16)
         ts(T.ff[:], T.o3[:], 4096.0, 0.5, OP.is_lt, OP.max, ["o30", "o31"], ["ff"])
         cp(T.nl[:], MN(t, 16, 24), [MNk[t][2]], ["nl"])
         for h in range(2):
@@ -613,10 +650,17 @@ def rank_program(g, core, T, topo):
             scat(T.ov, "ov", 0)
             scat(T.op_, "op", 1)
         aff("oh", T.oh[:], B[0][:, 128:256], [], ["oh"], [0])
-        mm(B[5][:, 0:8], T.iff[:], T.j16[:], True, False, ["iff", "j16"], 5, 4)
-        for r in range(16):
-            mm(B[5][:, 0:8], T.bk[:, 15 - r:143 - r], T.oh[:, r:128:16], False, r == 15, ["bk", "oh"], 5)
-        join(16)
+        if LM[1]:
+            mm(B[5][:, 0:8], T.ib[:], T.j16[:], True, False, ["ib", "j16"], 5)
+            for r in range(16):
+                mm(B[5][:, 0:8], T.sk[:, 15 - r:143 - r], T.oh[:, r:128:16], False, r == 15, ["bk", "oh"], 5)
+            join(17)
+        else:
+            mm(B[5][:, 128:256], T.oh[:], T.bk[:], True, True, ["bk", "oh"], 5)
+            tt(T.km[:], B[5][:, 128:256], T.mr[:], OP.mult, ["mr"], ["km"], [5])
+            mm(B[5][:, 0:8], T.ib[:], T.j16[:], True, False, ["ib", "j16"], 5)
+            mm(B[5][:, 0:8], T.km[:], T.b16[:], False, True, ["km", "b16"], 5)
+            join(2)
         cp(T.kl[:], B[5][:, 0:8], [], ["kl"], [5])
         tt(T.df[:], ind(T.xg[:], T.kl[:]), ZI(t), OP.subtract, xgk + ["kl", "z%d" % t], ["df"])
         act(ZO(t), T.df[:], AF.Abs, ["df"], ["zo%d" % t])

from concourse.bass import DstId, RemoteDMATransfer
from concourse.mybir import AluOpType as OP, ActivationFunctionType as AF, AxisListType as AX

F32, BF, F16, I32, U16 = "float32", "bfloat16", "float16", "int32", "uint16"
NT = 4
BIG = 8192.0
LV = (24, 24, 24, 24)
XS = 20
DQ = ((0, 2), (2, 3), (3, 4))
NI = (1, 2, 3)
LM = (1, 1)
ONV = ("ev", "z192")
DEC = ((2, 1), (3, 1), (2, 1), (3, 1), (4, 0), (5, 0), (4, 0), (5, 0))
KBT = 5.0
PEC = 0.55
GAT, SCA, HOP, FAR = 1.56, 3.5, 100.0, 2200.0


def _sb(n, d):
    return ("sbuf", [128, n], d)


SCRATCH = {
    "rv": _sb(1024, I32), "rp": _sb(1024, I32), "vd": _sb(1160, F32), "pd": _sb(1160, F32),
    "ov": _sb(1160, F32), "op_": _sb(1160, F32), "ox": _sb(1024, F32), "xw": _sb(6144, BF),
    "vni": _sb(8, I32), "pni": _sb(8, I32), "wi": _sb(4, I32), "wn": _sb(4, I32), "thi": _sb(128, I32),
    "thf": _sb(128, F32), "th16": _sb(128, F32), "tha": _sb(128, F32),
    "ci": _sb(16, I32), "cf": _sb(16, F32), "l16": _sb(16, F32), "m16": _sb(16, F32), "sg": _sb(16, F32),
    "pw": _sb(16, F32), "pw2": _sb(16, F32), "two": _sb(16, F32), "c16": _sb(8, F32), "jj": _sb(8, F32),
    "j32": _sb(8, F32), "j16": _sb(8, BF), "dump": _sb(16, F32), "bci": _sb(8, I32), "bc": _sb(8, U16),
    "g128": _sb(128, F32), "bw0": _sb(128, BF), "bw1": _sb(128, BF), "mr": _sb(128, BF), "sel": _sb(8, F32),
    "um": _sb(128, F32), "km": _sb(128, BF), "bk": _sb(128, BF), "blk": _sb(128, BF), "b16": _sb(8, BF), "kc": _sb(128, BF),
    "rs": _sb(128, F32), "ones": _sb(128, BF), "onef": _sb(128, F32), "ib": _sb(128, BF),
    "iff": _sb(128, F32), "nif": _sb(128, F16), "nbig": _sb(256, BF), "sc3": _sb(384, BF),
    "c48": _sb(64, BF), "bigc": _sb(8, BF), "w2": _sb(256, BF), "dk": _sb(2048, F16), "ee": _sb(2048, BF),
    "ft": _sb(1040, BF), "iot": _sb(4096, F32),
    "eq": ("sbuf", [128, 8, 8, 16], BF), "vl": _sb(64, U16), "er": _sb(1024, BF), "fu": _sb(128, BF),
    "x144": _sb(144, F32), "bs": _sb(144, BF), "sw0": _sb(144, BF), "sw1": _sb(144, BF), "sk": _sb(144, BF),
    "om": _sb(16, F32), "osc": _sb(16, U16), "nl": _sb(8, U16), "nx": _sb(8, U16),
    "o1": _sb(128, U16), "o2": _sb(128, U16), "o3": _sb(128, U16), "r1": _sb(128, F16), "r2": _sb(128, F16),
    "g2": _sb(2048, F16), "g3": _sb(2048, F16), "xg": _sb(2048, BF), "ab": _sb(2048, BF), "zt": _sb(128, BF),
    "ff": _sb(128, F32), "e4": _sb(128, F32), "nme": _sb(128, F32), "pm": _sb(128, F32),
    "near": _sb(128, BF), "ge": _sb(128, BF), "key": _sb(128, F32), "t1": _sb(128, F32), "ep": _sb(128, F32), "rr": _sb(256, F32),
    "oh": _sb(128, BF), "kl": _sb(8, U16), "df": _sb(128, BF), "tt": _sb(128, BF), "z192": _sb(128, BF),
    "ac": _sb(8, F32), "aq": _sb(8, BF), "iw": _sb(64, I32), "yl": _sb(16, U16), "ya": _sb(128, F32), "yb": _sb(128, F32),
    "zi": _sb(128 * NT, BF), "zo": _sb(128 * NT, BF), "fi": _sb(264 * NT, BF), "fo": _sb(264 * NT, BF),
    "mo": _sb(24 * NT, F32), "mn": _sb(24 * NT, F32), "ml": _sb(24 * NT, F32),
}
for _t in range(8):
    SCRATCH["b%d" % _t] = ("psum", [128, 512], F32)

NDMA = 24
SEMAPHORES = (["cV", "cS", "cP", "cG", "sent", "aw"] + ["d%d" % i for i in range(NDMA)]
              + [a + str(t) for a in ("az", "an", "al", "af") for t in range(1, NT)])


PUSH = {x.split(":")[0]: 100 * int(x.split(":")[1]) for x in """
sYvni.1:900 sYrv0.1:800 sYrv1.1:700 sYrp0.1:600 sYrp1.1:500 sYxa.1:400 sSpni.1:900 sSwi.1:800 sSz.1:700 sSthi.1:600
Vee.5:-79 Vq5.1:-48 sVpw.1:-35 Vnl.1:-146 Vnx.1:-43 Vv37.1:-89 Vmoc.1:-63 sVpwa.1:-68 sVci1.1:-61 Pfoo3.2:221 sVxe.2:-55 eVya.1:-40 Ve411.1:112 sVjj.1:-34 Vvd.1:-45 Vz92.1:-290 Pw21.2:-56 Stt.1:32 sSiff.1:-200 Pab06.17:62 Vui5.1:-66 Vnear6.1:152 sVw0.1:-7 sSfic7.1:202 Vop35.1:85 Vff.1:-54 sSdumpa.1:-87 sVblk.1:45 Vev5.1:21 Saq.1:-65 sVv37.1:26 Spb22.2:-52 sVrs.1:-41 Soh0.1:-47 Vee.10:38 sVenc11.2:-52 Vg31v.1:-51 eVyl.1:50 Sab1.1:97 Vxg2.1:63 sGiot4.1:38 sVsel.1:180 sVpwb.1:-105 Vee.14:-45 sVones.1:-46 Vo311.1:-62 Pfoo2.1:-60 Pw24.1:-45 sVbk.1:95 sVs1.1:-28 Vov13.1:-70 Vo1.1:64 Vg21v.1:137 Vum5.1:33 Szo.1:42 Seq32.1:-22 sVdk.8:19 sGkc.1:22 sVnif.1:-44 Vo300.1:50 Sg21s.1:35 Seq63.1:-24 Vnme.1:27 Vsq.1:-36 Seq02.1:12 sPonef6.1:-30 sVpwc.1:-70 Vom7.1:-85 Vo211.1:-47 ePib1.1:-30 Pfoo3.1:-8 Spb55.1:-30 Vee.9:-5 sSeq02.1:-42 sGl16.1:5 sVvd0.1:-40 sPfie2.1:-2
""".split()}


ORDER = "0=0>0H0J0?0B1H0@310I0A1J0M2R231D1G1F1L0K1I1E1O271N0L1K380C282A103611122B2C261A2D1M291P2E1Q2F2G1R132:1S240D141T252H1U2I2J2<1V150O2=161W1C172K2?39373:18203D4W0E3;213E2L500V4A19513F3R0F3S3T3340524@3<0P3U3=2M3V2N3W3G3>0G534B41444F4C5T421:430N544D4E454G0U1;550R3I575U2O560S0W5W4H4I2P1@595:2@585?1B465;5<1<5@4:5A485=1=5B3H5E5F4900473J5>5C5D5G5H3K1>5M5K5N4=1?5I3M3L5L4<613N4;5J3O4J64650T605O5V4>4K5P3P68623Q66634P696<676=4N6:4R2Q2W6>6;226C4S2U6F6@042V6E2S3?6?4L2;3@2T80306A2>4O6J3A4?326K6D6B34354Q6L7B7:6Q0Q7>7;4M6R7<7C7?7=7D7@4T6H7A6G6S6I4U7F7E4V5Q7G7P7K7H6T5R6M6V6N5S8:7I6O6P7L8;757J6U768?7M8@8A6W027N8C8I748B717O7Q8H8D8G7T7U728E7R8M708F8J8N737W8O8P8K81017S8S8Q8L8T8U8V77838R859894788W95797V96999082868<9<9=8=8>87849:889@89979;9A9>069D9E9?9B919C9F923B03089K;09H9N9G939R9M9Q3C9L;89O9S9I9P9T9J:1:B:2:C:3:4:E:F:6:J:K:D9U:N:L:O9V:G:M9W:P:;;B:S:H:R:0:I:T:=:5:Q:<;C:U:::V;G:W;1;H;I;4;5;J:>;K;P:7;O;L:9;7;2;Q:805;M;:;R;9;U;3;V<<:?;N;S;T;W<=;;<0<4<1<3;=<I<2;<;><@<5<?<A;D;6:@<><6<7;?<D;E;F<B<8;@<H;A<E<C<F:A<9<L<G<J<M<K>7<:<N<;<S070<<U<P<V<O<T=1=2<W0:=3<Q=0>==4<R=9=I=Q=5=J=R=K=M=N=L=S>I>J=U=6=V=T=7=:=W>2=O>?=;>1=P=<>3=>>0?E=F>4>N=D>5>P?F=E>8>O>Q>R=8>6?I>;><>W>V=C>S>9>>==?0?1>T>@?5?4=@09?C>U>B>A?6=B>D>C?2?3?J?<?7?==?>:?G?8?;=A?D?:?T>E?9?H?P>F?S=G?O?M?>?K?U=H??>G?W>H?Q?V@0?R?N?L@1@3?@@B@4@2@:@50;@=@<@;AH@7@C@6A6?A@>>K@8@?>L>M@9@@@P@H@F@L@Q@I@M@J@K@R@S?B@T@N@UA1@VA0A2@AA;@DA3A4@O@EA5@GA7@WA8AIA9A<A:AJABA=A>A?ACA@ADAEAAAFAGAK"


def planner(ops):
    n = len(ops)
    lastw, readers, bank = {}, {}, {}
    pre = [dict() for _ in ops]
    sends = {o["tag"]: i for i, o in enumerate(ops) if o["kind"] == "r"}
    for i, o in enumerate(ops):
        def dep(j, raw):
            same = ops[j]["q"] == o["q"] and ops[j]["kind"] == "c" and o["kind"] == "c"
            pre[i][j] = max(pre[i].get(j, 0), ops[j]["lat"] + (HOP if raw or not same else 0))
        if o["kind"] == "a":
            dep(sends[o["tag"]], True)
        for k in o["r"]:
            if k in lastw:
                dep(lastw[k], True)
        for k in o["w"]:
            for j in readers.get(k, []):
                dep(j, True)
            if k in lastw:
                dep(lastw[k], False)
        for k in o["b"]:
            if k in bank:
                dep(bank[k], False)
            bank[k] = i
        for k in o["r"]:
            readers.setdefault(k, []).append(i)
        for k in o["w"]:
            lastw[k] = i
            readers[k] = []
        pre[i].pop(i, None)
    suc = [[] for _ in ops]
    for i in range(n):
        for j in pre[i]:
            suc[j].append(i)
    dur = [o["dur"] for o in ops]
    que = [o["q"] if o["kind"] != "a" else "A" for o in ops]

    def tails(order, after):
        tail = [0.0] * n
        for i in reversed(order):
            t = ops[i]["lat"]
            for j in suc[i]:
                t = max(t, pre[j][i] + dur[j] + tail[j])
            if after.get(i) is not None:
                t = max(t, dur[after[i]] + tail[after[i]])
            tail[i] = t
        return tail

    def plan(tail):
        wait = [len(p) for p in pre]
        rdy = [0.0] * n
        pool = {q: [] for q in set(que)}
        free = {q: 0.0 for q in pool}
        for i in range(n):
            if not wait[i]:
                pool[que[i]].append(i)
        order, after, last, span = [], {}, {}, 0.0
        while len(order) < n:
            t, q = min((max(free[q], min(rdy[i] for i in p)), q) for q, p in pool.items() if p)
            p = pool[q]
            x = max((i for i in p if rdy[i] <= t), key=lambda i: tail[i])
            best = None
            for y in p:
                if t < rdy[y] < t + dur[x] and tail[y] > tail[x]:
                    gain = t + dur[x] + dur[y] + tail[y] - max(rdy[y] + dur[y] + tail[y], rdy[y] + dur[y] + dur[x] + tail[x])
                    if gain > 0 and (best is None or gain > best[0]):
                        best = (gain, y)
            if best:
                fit = [i for i in p if rdy[i] <= t and t + dur[i] <= rdy[best[1]]]
                x = max(fit, key=lambda i: tail[i]) if fit else best[1]
            p.remove(x)
            e = max(t, rdy[x]) + dur[x]
            if q != "A":
                free[q] = e
                if q in last:
                    after[last[q]] = x
                last[q] = x
            order.append(x)
            span = max(span, e + ops[x]["lat"])
            for j in suc[x]:
                rdy[j] = max(rdy[j], e + pre[j][x])
                wait[j] -= 1
                if not wait[j]:
                    pool[que[j]].append(j)
        return span, order, after

    tail = tails(plan([0.0] * n)[1], {})
    return (lambda push: plan([x + push.get(o["cls"], 0) for x, o in zip(tail, ops)])), pre


def arrange(ops):
    if ORDER:
        order = [40 * (ord(ORDER[i]) - 48) + ord(ORDER[i + 1]) - 48 for i in range(0, len(ORDER), 2)]
    else:
        order = planner(ops)[0](PUSH)[1]
    return [ops[i] for i in order if ops[i]["kind"] == "a"] + [ops[i] for i in order if ops[i]["kind"] != "a"]


def emit(g, T, ops):
    Q = {"V": g.vector, "S": g.scalar, "P": g.tensor, "G": g, "Y": g.sync}
    lastw, readers, bank, deps = {}, {}, {}, []
    for i, o in enumerate(ops):
        d = set()
        own = o["q"] if o["kind"] == "c" else None
        for k in o["r"]:
            if k in lastw:
                d.add(lastw[k])
        for k in o["w"]:
            d.update(readers.get(k, []))
            if k in lastw and (ops[lastw[k]]["kind"] != "c" or ops[lastw[k]]["q"] != own):
                d.add(lastw[k])
        for k in o["b"]:
            if k in bank and ops[bank[k]]["q"] != own:
                d.add(bank[k])
            bank[k] = i
        for k in o["r"]:
            readers.setdefault(k, []).append(i)
        for k in o["w"]:
            lastw[k] = i
            readers[k] = []
        d.discard(i)
        deps.append(d)
    know = {q: {} for q in Q}
    done = []
    need = []
    for i, o in enumerate(ops):
        kn = know[o["q"]] if o["kind"] != "a" else {}
        mine = []
        for j in sorted(deps[i], reverse=True):
            key = ops[j]["q"] if ops[j]["kind"] == "c" else ("x", j)
            if kn.get(key, -1) >= j:
                continue
            mine.append(j)
            for k2, v2 in done[j].items():
                if kn.get(k2, -1) < v2:
                    kn[k2] = v2
        need.append(mine)
        dn = dict(kn)
        dn[o["q"] if o["kind"] == "c" else ("x", i)] = i
        done.append(dn)
    awaited = set(j for m in need for j in m)
    count = {q: 0 for q in Q}
    at = {}
    nd = [0]
    sent = [0]
    open_ = {}
    for i, o in enumerate(ops):
        if o["kind"] == "a":
            at[i] = (o["sem"], o["n"])
            open_[i] = at[i]
            continue
        q = Q[o["q"]]
        for j in need[i]:
            q.wait_ge(at[j][0], at[j][1])
            open_.pop(j, None)
        ins = o["f"]()
        if o["kind"] == "c":
            if i in awaited:
                count[o["q"]] += 1
                s = T.sem["c" + o["q"]]
                ins.then_inc(s, 1)
                at[i] = (s, count[o["q"]])
        elif o["kind"] == "d":
            s = T.sem["d%d" % nd[0]]
            nd[0] += 1
            ins.then_inc(s, 16)
            at[i] = (s, 16)
            open_[i] = at[i]
        else:
            sent[0] += o["n"]
    g.wait_ge(T.sem.sent, sent[0])
    for s, n in open_.values():
        g.wait_ge(s, n)


def rank_program(g, core, T, topo):
    rank = T.rank_of(core)
    if rank is None:
        return
    N = len(T.cores)
    nxt, nx2, prv, pr2 = (T.cores[(rank + k) % N] for k in (1, 2, -1, -2))
    ops, sect, seen = [], ["s"], {}
    V, S, P = g.vector, g.scalar, g.tensor

    def op(q, f, r=(), w=(), b=(), kind="c", n=0, sem=None, dur=64.0, lat=0.0, tag=None):
        nm = (list(w) + [tag or ""] + list(r))[0 if w else (0 if tag else 1) if (tag or r) else 0]
        for a in ("vl", "fo", "fi", "mo", "zo", "z", "m", "f", "mn", "ml", "fic", "foc", "foe", "foo", "fie", "fio"):
            if nm[:len(a)] == a and nm[len(a):len(a) + 1].isdigit():
                nm = a + nm[len(a) + 1:]
        nm = sect[0] + q + nm + "".join(str(x) for x in b)
        seen[nm] = seen.get(nm, 0) + 1
        ops.append({"cls": nm + "." + str(seen[nm]), "q": q, "f": f, "r": list(r), "w": list(w), "b": list(b), "kind": kind, "n": n, "sem": sem,
                    "dur": dur, "lat": lat, "tag": tag})

    def els(a):
        m = 1
        for x in a.shape[1:]:
            m *= x
        return m

    def ind(win, off):
        return (win.indirect(off), 16 * els(off))

    def vop(make, out, a, r, w, b, f):
        if isinstance(out, tuple):
            out, dur = out[0], 50.0 + SCA * out[1]
        elif isinstance(a, tuple):
            a, dur = a[0], 50.0 + GAT * a[1]
        else:
            dur = max(64.0, f * els(out))
        op("V", lambda: make(out, a), r, w, b, dur=dur)

    def ts(out, in0, s1, s2, o0, o1, r, w, b=(), f=1.0):
        if o1 is None:
            vop(lambda o, a: V.tensor_scalar(o, a, s1, None, o0), out, in0, r, w, b, f)
        else:
            vop(lambda o, a: V.tensor_scalar(o, a, s1, s2, o0, o1), out, in0, r, w, b, f)

    def tt(out, a, c, o, r, w, b=()):
        vop(lambda x, y: V.tensor_tensor(x, y, c, o), out, a, r, w, b, 1.0 if b else 2.0)

    def cp(out, a, r, w, b=(), f=1.0):
        vop(lambda x, y: V.tensor_copy(x, y), out, a, r, w, b, f)

    def ms(out, c, w, r=(), f=0.5):
        op("V", lambda: V.memset(out, c), r, w, dur=max(64.0, f * els(out)))

    def act(out, a, func, r, w, b=(), bias=0.0, scale=1.0, acc=None):
        dur = 65.0 + els(out)
        if isinstance(a, tuple):
            a, dur = a[0], 65.0 + GAT * a[1]
        op("S", lambda: S.activation(out, a, func, bias=bias, scale=scale, accum_out=acc), r, w, b, dur=dur)

    def aff(name, out, a, r, w, b=(), bias=0.0, scale=1.0, f=1.0):
        if name in ONV:
            ts(out, a, scale, bias, OP.mult, OP.add, r, w, b, f)
        else:
            act(out, a, AF.Identity, r, w, b, bias=bias, scale=scale)

    def mm(out, l, rh, st, sp, r, bk, f=1.0):
        op("P", lambda: P.matmul(out, l, rh, st, sp), r, (), [bk], dur=PEC * f * max(min(64, els(l)), els(rh)))

    def join(k):
        part_ = ops[-k:]
        del ops[-k:]
        op("P", lambda: [o["f"]() for o in part_][-1], sorted(set(x for o in part_ for x in o["r"])), (), part_[0]["b"],
           dur=sum(o["dur"] for o in part_))

    def iota(out, pat, base, cm, w, fl=True):
        if fl:
            op("G", lambda: g.iota(out, pat, base, cm, allow_small_or_imprecise_dtypes=True), (), w, dur=130.0 + 2 * els(out))
        else:
            op("G", lambda: g.iota(out, pat, base, cm), (), w, dur=130.0 + 2 * els(out))

    def asel(out, a, pat, c, base, cm, r, w):
        op("G", lambda: g.affine_select(out, a, pat, c, 0.0, base, cm), r, w, dur=170.0 + 2 * els(out))

    def dma(q, out, a, r, w, kb=0):
        e = {"Y": g.sync, "S": S, "G": g}[q]
        op(q, lambda: e.dma_start(out, a), r, w, kind="d", dur=60.0 + KBT * kb, lat={"z0": 3500.0, "thi": 4700.0}.get((list(w) + [0])[0], 2100.0))

    def eng(a, c):
        return len(topo.engines(a, c))

    def send(src, dests, r, tag):
        trs, n = [], 0
        share = len(dests)
        for i, (c, dst, sem) in enumerate(dests):
            es = topo.engines(core, c)
            k = len(es) // share
            m = sum(1 << e for e in es[i * k:(i + 1) * k])
            rid, pid = topo.addr(c)[:2]
            trs.append((c, dst, sem, m, rid, pid))
            n += k
        if share == 1:
            c, dst, sem, m, rid, pid = trs[0]
            op("G", lambda: g.remote_dma(dst, src, sem, T.sem.sent, pid, rid, m), r, kind="r", n=n, dur=600.0, lat=FAR - 600.0, tag=tag)
        else:
            op("G", lambda: g.remote_dma_fused(
                [RemoteDMATransfer(dst_ids=[DstId(rid=x[4], pnc=x[5])], dma_engine_mask=x[3], remote_sem=x[2], src=src, dst=x[1])
                 for x in trs], local_sem=T.sem.sent), r, kind="r", n=n, dur=600.0, lat=FAR - 600.0, tag=tag)

    def arrive(sem, n, w, tag):
        op("G", None, (), w, kind="a", n=n, sem=sem, dur=0.0, tag=tag)

    B = [T["b%d" % i] for i in range(8)]

    def part(buf, width):
        return lambda t, a=0, e=width, s=1: buf[:, width * t + a:width * t + e:s] if s > 1 else buf[:, width * t + a:width * t + e]

    ZI, ZO, FI, FO, MO, ML = part(T.zi, 128), part(T.zo, 128), part(T.fi, 264), part(T.fo, 264), part(T.mo, 24), part(T.ml, 24)
    mn_ = part(T.mn, 24)

    def MN(t, a=0, e=24):
        return MO(0, a, e) if t == 0 else mn_(t, a, e)

    MNk = [["mo0a", "mo0b", "mo0c"]] + [["mn%d" % t] * 3 for t in range(1, NT)]
    IW = {k: T.iw[:, 8 * i:8 * i + 8] for i, k in enumerate(("ui", "u12", "m5", "sq", "q5", "v37", "s1", "vw"))}
    arrive(T.sem.aw, eng(nxt, core), ["wn"], "w")
    for t in range(1, NT):
        arrive(T.sem["az%d" % t], eng(prv, core), ["z%d" % t], "z%d" % (t - 1))
        arrive(T.sem["af%d" % t], eng(prv, core), ["fic%d" % t, "fie%d" % t, "fio%d" % t], "f%d" % (t - 1))
        arrive(T.sem["an%d" % t], eng(prv, core) // (2 if t < NT - 1 else 1), ["mn%d" % t], "m%d" % t)
        arrive(T.sem["al%d" % t], eng(prv, core) if t == 1 else eng(pr2, core) // 2, ["ml%d" % t], "m%d" % (t - 1))

    dma("Y", T.vni[:], T.vn[:], (), ["vni"])
    dma("S", T.pni[:], T.pn[:], (), ["pni"])
    dma("S", T.wi[:, 0:1], T.wt[:], (), ["wi"])
    dma("S", ZI(0), T.z[:], (), ["z0"])
    dma("S", T.thi[0:1, :], T.th[:], (), ["thi"])
    for raw, src, k in ((T.rv, T.vdir, "rv"), (T.rp, T.pdir, "rp")):
        for h in range(2):
            dma("Y", raw[:, 512 * h:512 * h + 512], src[:, 512 * h:512 * h + 512], (), [k + str(h)], 256)
    dma("Y", T.xw[:, 0:1024], T.xl[:, 0:1024], (), ["xa"], 256)
    dma("Y", T.xw[:, 1024:4096], T.xl[:, 1024:4096], (), ["xb"], 768)

    pm, gb, me, mo, wc, w0, w1 = (T.cf[:, i:i + 1] for i in range(7))
    ms(T.ones[:], 1.0, ["ones"])
    iota(T.ci[:, 0:1], [[0, 1]], 0, 1, ["ci0"], False)
    iota(T.l16[:], [[1, 16]], 0, 0, ["l16"])
    asel(T.ib[:], T.ones[:], [[-1, 128]], OP.is_equal, 0, 1, ["ones"], ["ib"])
    iota(T.c16[:], [[16, 8]], 0, 0, ["c16"])
    iota(T.g128[:], [[16, 8], [0, 16]], 0, 0, ["g128"])
    iota(T.kc[:], [[0, 8], [1, 16]], 0, 0, ["kc"])
    iota(T.bci[:], [[16, 8]], 15, 0, ["bci"], False)
    IOT = ["iot%d" % i for i in range(8)]
    for i in range(8):
        if i in NI:
            act(T.iot[:, 512 * i:512 * i + 512], T.iot[:, 0:512], AF.Identity, ["iot0"], [IOT[i]], bias=512.0 * i)
        else:
            iota(T.iot[:, 512 * i:512 * i + 512], [[1, 512]], 4096 + 512 * i, 0, [IOT[i]])
    for q in range(4):
        for k in range(4 * q, 4 * q + 4):
            ts(T.ee[:, k:2048:16], T.ib[:], -1.0, None, OP.mult, None, ["ib"], ["ee"], f=0.5)
    for q in range(2):
        cp(T.xw[:, 4096 + 1024 * q:5120 + 1024 * q:2], T.xw[:, 512 * q:512 * q + 512], ["xa"], ["xe2"], f=0.5)
        iota(T.xw[:, 4097 + 1024 * q:5120 + 1024 * q:2], [[0, 512]], 0, 0, ["xe"])
    ms(T.ft[:, 0:2], -1.0, ["ft"])
    ms(T.two[:], 2.0, ["two"])
    ts(T.ci[:, 1:2], T.ci[:, 0:1], 15, None, OP.bitwise_and, None, ["ci0"], ["ci1"])
    ts(T.ci[:, 2:3], T.ci[:, 0:1], 16, None, OP.bitwise_and, None, ["ci0"], ["ci2"])
    ms(T.vd[:, 0:1], 4096.0, ["vd0"])
    cp(pm, T.ci[:, 1:2], ["ci1"], ["pm_"])
    ms(T.pd[:, 0:1], 4096.0, ["pd0"])
    ts(T.m16[:], T.l16[:], pm, None, OP.is_equal, None, ["l16", "pm_"], ["m16"])
    ts(me, T.ci[:, 2:3], 0.0, None, OP.is_equal, None, ["ci2"], ["me"])
    ts(T.sg[:], T.m16[:], -2.0, 1.0, OP.mult, OP.add, ["m16"], ["sg"])
    ts(mo, T.ci[:, 2:3], 0.0, None, OP.is_gt, None, ["ci2"], ["mo"])
    tt(gb, T.ci[:, 0:1], T.ci[:, 1:2], OP.subtract, ["ci0", "ci1"], ["gb"])
    for l in range(10):
        act(T.ft[:, 1 + 2 ** l:1 + 2 ** (l + 1)], T.ft[:, 1:1 + 2 ** l], AF.Copy, ["ft", "sg"], ["ft"], scale=T.sg[:, l:l + 1])
    ts(T.nbig[:, 0:128], T.ib[:], -BIG, None, OP.mult, None, ["ib"], ["nbig"], f=0.5)
    ms(T.bigc[:], BIG, ["bigc"])
    ts(ML(0, 0, 8), T.vni[:], 1.0, None, OP.add, None, ["vni"], ["ml0"])
    ts(ML(0, 8, 16), T.pni[:], 1.0, None, OP.add, None, ["pni"], ["ml0"])
    ts(T.jj[:], T.c16[:], pm, None, OP.add, None, ["c16", "pm_"], ["jj"])
    ts(T.blk[:], T.g128[:], gb, None, OP.is_equal, None, ["g128", "gb"], ["blk"])
    if 0 in LM:
        ts(T.mr[:], T.kc[:], pm, None, OP.is_equal, None, ["kc", "pm_"], ["mr"], f=0.5)
    if 1 in LM:
        iota(T.x144[:], [[1, 144]], -15, 0, ["x144"])
        ts(T.bs[:], T.x144[:], gb, None, OP.is_equal, None, ["x144", "gb"], ["bs"])
    cp(w0, T.wi[:, 0:1], ["wi"], ["w0"])
    cp(w1, T.wn[:, 0:1], ["wn"], ["w1"])
    ts(T.j32[:], T.jj[:], 32.0, None, OP.mult, None, ["jj"], ["j32"])
    if LM[0]:
        ts(T.sw0[:], T.bs[:], w0, None, OP.mult, None, ["bs", "w0"], ["bw0"], f=0.5)
        ts(T.sw1[:], T.bs[:], w1, None, OP.mult, None, ["bs", "w1"], ["bw1"], f=0.5)
    else:
        cp(T.sel[:], T.blk[:, 0:128:16], ["blk"], ["sel"])
        ts(T.bw0[:], T.blk[:], w0, None, OP.mult, None, ["blk", "w0"], ["bw0"], f=0.5)
        ts(T.bw1[:], T.blk[:], w1, None, OP.mult, None, ["blk", "w1"], ["bw1"], f=0.5)
    if LM[1]:
        ts(T.sk[:], T.bs[:], pm, None, OP.mult, None, ["bs", "pm_"], ["bk"], f=0.5)
    else:
        ts(T.bk[:], T.blk[:], pm, 0.0625, OP.mult, OP.mult, ["blk", "pm_"], ["bk"], f=0.5)
    send(T.wi[:, 0:1], [(prv, T.wn[:, 0:1], T.sem.aw)], ["wi"], "w")
    for k in range(16):
        ts(T.dk[:, 128 * k:128 * k + 128], T.ib[:], T.m16[:, k:k + 1], None, OP.mult, None, ["ib", "m16"], ["dk"], f=0.5)
    op("V", lambda: V.tensor_tensor_scan(T.pw[:], T.two[:], T.ones[:, 0:16], 0.5, OP.mult, OP.mult), ["two", "ones"], ["pw"])
    ms(T.c48[:], 32.0, ["c48"])
    ms(T.pw[:, 10:11], -4096.0, ["pwa"], ["pw"])
    ms(T.pw[:, 11:12], -1024.0, ["pwb"], ["pw"])
    ms(T.pw[:, 12:13], 1.0, ["pwc"], ["pw"])
    ms(T.pw[:, 13:16], 0.0, ["pwd"], ["pw"])
    ts(T.b16[:], T.blk[:, 0:128:16], 16.0, None, OP.mult, None, ["blk"], ["b16"])
    tt(T.pw2[:], T.pw[:], T.m16[:], OP.mult, ["pw", "pwa", "pwb", "pwc", "pwd", "m16"], ["pw2"])
    ms(T.onef[0:1, :], 1.0, ["onef"], f=1.0)
    op("V", lambda: V.tensor_reduce(wc, T.pw2[:], AX.X, OP.add), ["pw2"], ["wc"])
    ts(T.thf[0:1, :], T.thi[0:1, :], 16.0, None, OP.mult, None, ["thi"], ["thf"])
    ts(T.w2[:, 0:128], T.blk[:], wc, None, OP.mult, None, ["blk", "wc"], ["w2"], f=0.5)
    ts(T.w2[:, 128:256], T.blk[:], wc, 0.5, OP.mult, OP.mult, ["blk", "wc"], ["w2"], f=0.5)
    act(T.nbig[:, 128:256], T.ib[:], AF.Copy, ["ib"], ["pbig"], scale=BIG)
    cp(T.nif[:], T.ib[:], ["ib"], ["nif"], f=0.5)
    act(T.iff[:], T.ib[:], AF.Copy, ["ib"], ["iff"])
    act(T.j16[:], T.jj[:], AF.Copy, ["jj"], ["j16"], scale=16.0)
    act(T.dump[:, 0:8], T.jj[:], AF.Identity, ["jj"], ["dumpa"], bias=1025.0)
    act(T.dump[:, 8:16], T.jj[:], AF.Identity, ["jj"], ["dumpb"], bias=1025.0)
    mm(B[6][:, 0:128], T.onef[0:1, :], T.thf[0:1, :], True, True, ["onef", "thf"], 6, 4)
    act(T.tha[:], B[6][:, 0:128], AF.Copy, [], ["tha"], [6])
    act(T.th16[:], B[6][:, 0:128], AF.Identity, [], ["th16"], [6], bias=790528.0)
    ts(T.rs[:], T.kc[:], 0.0, 65536.0, OP.is_equal, OP.mult, ["kc"], ["rs"])
    cp(T.bc[:], T.bci[:], ["bci"], ["bc"])
    for i, s in enumerate((64.0, 4096.0, 262144.0)):
        ts(T.sc3[:, 128 * i:128 * i + 128], T.ib[:], s, None, OP.mult, None, ["ib"], ["sc3"], f=0.5)

    def encode(raw, tab, k, h, b0):
        rk = "r" + k[0] + str(h)
        ts(B[b0][:], raw[:, 512 * h:512 * h + 512], 4096.0, 0.0, OP.subtract, OP.max, [rk], ["enc%d" % b0], [b0])
        tt(tab[:, 1 + 512 * h:513 + 512 * h], raw[:, 512 * h:512 * h + 512], B[b0][:], OP.add, [rk, "enc%d" % b0], [k], [b0])

    def chain(s):
        z, zk = (ZI, "z0") if s == 0 else (ZO, "zo%d" % (s - 1))
        zs = max(s - 1, 0)
        bw, bwk = (T.bw0, "bw0") if s == 0 else (T.bw1, "bw1")
        vo, vk = (ML(0, 0, 8), "ml0") if s == 0 else (MN(s - 1, 0, 8), MNk[s - 1][0])
        m, bk = "mo%d" % s, 5 if s else 7
        if LM[0]:
            sw = T.sw1 if s else T.sw0
            for r in range(16):
                mm(B[bk][:, 8:16], sw[:, 15 - r:143 - r], z(zs, r, 128, 16), r == 0, r == 15, [zk, bwk], bk)
            join(16)
        else:
            mm(B[bk][:, 128:256], z(zs), bw[:], True, True, [zk, bwk], bk)
            tt(T.um[:], B[bk][:, 128:256], T.mr[:], OP.mult, ["mr"], ["um"], [bk])
            mm(B[bk][:, 8:16], T.um[:], T.sel[:], True, True, ["um", "sel"], bk, 4)
        aff("mob", MO(s, 8, 16), vo, [vk], [m + "b"])
        cp(IW["ui"], B[bk][:, 8:16], [], ["ui"], [bk])
        ts(IW["v37"], vo, 37.0, -37.0, OP.mult, OP.add, [vk], ["v37"])
        ts(IW["u12"], IW["ui"], 4095, None, OP.bitwise_and, None, ["ui"], ["u12"])
        ts(IW["m5"], IW["ui"], 31, None, OP.bitwise_and, None, ["ui"], ["m5"])
        tt(IW["sq"], IW["u12"], IW["u12"], OP.mult, ["u12"], ["sq"])
        tt(MO(s, 16, 24), IW["m5"], T.j32[:], OP.add, ["m5", "j32"], [m + "c"])
        ts(IW["q5"], IW["sq"], 5, None, OP.arith_shift_right, None, ["sq"], ["q5"])
        tt(IW["s1"], IW["q5"], IW["v37"], OP.add, ["q5", "v37"], ["s1"])
        ts(IW["vw"], IW["s1"], 1023, None, OP.bitwise_and, None, ["s1"], ["vw"])
        ts(MO(s, 0, 8), IW["vw"], 1.0, None, OP.add, None, ["vw"], [m + "a"])
        ks = [m + "a", m + "b", m + "c"]
        if s == 0:
            send(MO(s), [(nxt, ML(1), T.sem.al1)], ks, "m0")
        elif s < NT - 1:
            send(MO(s), [(nxt, MN(s), T.sem["an%d" % s]), (nx2, ML(s + 1), T.sem["al%d" % (s + 1)])], ks, "m%d" % s)
        else:
            send(MO(s), [(nxt, MN(s), T.sem["an%d" % s])], ks, "m%d" % s)

    def lists(t):
        cp(T.vl[:, 16 * t:16 * t + 16], ML(t, 0, 16), ["ml%d" % t], ["vl%d" % t])

    def repeats(F, buf, fk, t, h, bk):
        l, k, w = T.vl[:, 16 * t + 8 * h:16 * t + 8 * h + 8], "vl%d" % t, T.ft[:, 0:1025]
        if "fu" in ONV:
            act(T.fu[:], ind(w, l), AF.Copy, [k, "ft"], ["fu"])
            ts(F(t, 8, 136), T.fu[:], me, None, OP.mult, None, ["fu", "me"], [fk + "e%d" % t], f=0.5)
            ts(F(t, 136, 264), T.fu[:], mo, None, OP.mult, None, ["fu", "mo"], [fk + "o%d" % t], f=0.5)
        else:
            act(F(t, 8, 136), ind(w, l), AF.Copy, [k, "ft", "me"], [fk + "e%d" % t], scale=me)
            act(F(t, 136, 264), ind(w, l), AF.Copy, [k, "ft", "mo"], [fk + "o%d" % t], scale=mo)
        for gg in range(8):
            c0 = 264 * t + (136 if gg % 2 else 8)
            f = buf[32 * (gg // 2):32 * (gg // 2) + 32, c0:c0 + 128]
            o = B[bk + gg // 4][:, 128 * (gg % 4):128 * (gg % 4) + 128]
            mm(o, f, f, True, True, [fk + ("o%d" if gg % 2 else "e%d") % t], bk + gg // 4)
            if gg % 4 == 1:
                ops[-1]["w"] = ["tile%d" % (gg // 4)]
            if gg % 4 == 2:
                ops[-1]["r"].append("tile%d" % (gg // 4))
        for q in range(2):
            act(T.er[:, 512 * q:512 * q + 512], B[bk + q][:], AF.Relu, [], ["er%d" % q], [bk + q], bias=-15.0)
        for gg in range(8):
            asel(T.eq[:, :, gg, :], T.er[:, 128 * gg:128 * gg + 128], [[1, 128]], OP.is_gt, 0, -1, ["er%d" % (gg // 4)], ["eq%d" % gg])
        for c in range(8):
            mm(B[7][:, 8 + c:9 + c], T.eq[:, c, :, :], T.bigc[:, 0:1], True, True, ["eq%d" % i for i in range(8)] + ["bigc"], 7)
        join(8)
        aff("cnt", F(t, 0, 8), B[7][:, 8:16], [], [fk + "c%d" % t], [7])
        if fk == "fo" and t < NT - 1:
            send(F(t), [(nxt, FI(t + 1), T.sem["af%d" % (t + 1)])], ["foc%d" % t, "foe%d" % t, "foo%d" % t], "f%d" % t)

    def targets(t):
        mm(B[7][:, 16:32], T.iff[:], ML(t, 0, 16), True, False, ["iff", "ml%d" % t], 7, 4)
        for h in range(2):
            mm(B[7][:, 16 + 8 * h:24 + 8 * h], T.ib[:], FI(t, 0, 8), False, False, ["ib", "fic%d" % t], 7)
            mm(B[7][:, 16 + 8 * h:24 + 8 * h], T.ib[:], FO(t, 0, 8), False, h == 1, ["ib", "foc%d" % t], 7)
        join(5)
        tt(T.om[:], B[7][:, 16:32], T.dump[:], OP.min, ["dumpa", "dumpb"], ["om"], [7])
        cp(T.osc[:], T.om[:], ["om"], ["osc"])

    def look(tab, k, off, ok, gbuf, gk, h, lv, rbuf, rk, c0, last):
        a, m, e = 64 * h, 64 * h + lv, 64 * h + 64
        w = tab[:, 0:1025]
        act(gbuf[:, 16 * m:16 * e], ind(w, off[:, m:e]), AF.Identity, [k, k + "0", ok], [gk + "s"], bias=-2048.0)
        ts(gbuf[:, 16 * a:16 * m], ind(w, off[:, a:m]), -2048.0, None, OP.add, None, [k, k + "0", ok], [gk + "v"])
        o = B[h][:, c0:c0 + 64]
        mm(o, T.nif[:], rbuf[:, 64 * h:64 * h + 64], True, False, ["nif", rk], h)
        if last:
            mm(o, T.ones[:], T.c48[:], False, False, ["ones", "c48"], h)
        for i in range(16):
            mm(o, T.dk[:, 128 * i:128 * i + 128], gbuf[:, 1024 * h + i:1024 * h + 1024:16], False, i == 15, ["dk", gk + "v", gk + "s"], h)
        join(16)

    XK = ["xa", "xb", "xe", "xe2"]
    xgk = ["xg0", "xg1", "xgs", "xg2", "xg3"]

    def scat(tab, k, h):
        tt(ind(tab[:, 0:1153], T.osc[:, 8 * h:8 * h + 8]), T.ep[:], T.rr[:, 128 * h:128 * h + 128], OP.max,
           ["ep", "rr%d" % h, "osc"] + [k + str(i) for i in range(4)], [k])

    def decode(when):
        for i, (bk, wh) in enumerate(DEC):
            if wh == when:
                tab, k, out, ok = ((T.vd, "vd", T.ov, "ov"), (T.pd, "pd", T.op_, "op"))[i // 4]
                a, o = tab[:, 1 + 256 * (i % 4):257 + 256 * (i % 4)], out[:, 1 + 256 * (i % 4):257 + 256 * (i % 4)]
                act(B[bk][:, 0:256], a, AF.Relu, [k], ["pb%d" % bk], [bk], scale=0.5, bias=-2048.0)
                tt(o, a, B[bk][:, 0:256], OP.subtract, [k, "pb%d" % bk], [ok + str(i % 4)], [bk])

    lists(0)
    chain(0)
    repeats(FI, T.fi, "fi", 0, 1, 2)
    repeats(FO, T.fo, "fo", 0, 0, 4)
    for h in range(2):
        encode(T.rv, T.vd, "vd", h, h)
    for h in range(2):
        encode(T.rp, T.pd, "pd", h, h)

    for t in range(NT):
        vl = T.vl[:, 16 * t:16 * t + 8]
        sect[0] = ""
        seen.clear()
        ts(T.o1[:], ind(T.vd[:, 0:1025], vl), 4094.0, 0.5, OP.subtract, OP.mult, ["vd", "vd0", "vl%d" % t], ["o1"])
        ts(T.r1[:], ind(T.vd[:, 0:1025], vl), 4096.0, 2048.0, OP.min, OP.subtract, ["vd", "vd0", "vl%d" % t], ["r1"])
        for h in range(2):
            look(T.pd, "pd", T.o1, "o1", T.g2, "g2%d" % h, h, LV[h], T.r1, "r1", 0, False)
            ts(T.o2[:, 64 * h:64 * h + 64], B[h][:, 0:64], 4094.0, 0.5, OP.subtract, OP.mult, [], ["o2%d" % h], [h])
            ts(T.r2[:, 64 * h:64 * h + 64], B[h][:, 0:64], 4096.0, 2048.0, OP.min, OP.subtract, [], ["r2%d" % h], [h])
        for h in range(2):
            look(T.vd, "vd", T.o2, "o2%d" % h, T.g3, "g3%d" % h, h, LV[2 + h], T.r2, "r2%d" % h, 64, True)
            ts(T.o3[:, 64 * h:64 * h + 64], B[h][:, 64:128], -4096.0, None, OP.add, None, [], ["o3%d" % h], [h])
        targets(t)
        mm(B[6][:, 256:384], ZI(t), T.ib[:], True, True, ["z%d" % t, "ib"], 6)
        aff("zt", T.zt[:], B[6][:, 256:384], [], ["zt"], [6])
        if t == NT - 1:
            decode(0)
        act(T.xg[:, 16 * (64 - XS):1024], ind(T.xw[:], T.o3[:, 64 - XS:64]), AF.Copy, XK + ["o30"], ["xgs"])
        mm(B[6][0:32 * DQ[0][1], 0:128], T.ib[:, 0:32 * DQ[0][1]], T.kc[:], True, False, ["ib", "kc"], 6)
        for q in range(4):
            a, e = 32 * q, (64 - XS if q == 1 else 32 * q + 32)
            cp(T.xg[:, 16 * a:16 * e], ind(T.xw[:], T.o3[:, a:e]), XK + ["o3%d" % (q // 2)], ["xg%d" % q])
            mm(B[2 + q][:], T.zt[:], T.ee[:, 512 * q:512 * q + 512], True, False, ["zt", "ee"], 2 + q)
            mm(B[2 + q][:], T.ib[:], T.xg[:, 512 * q:512 * q + 512], False, True, ["ib", "xg%d" % q] + (["xgs"] if q == 1 else []), 2 + q)
            act(T.ab[:, 512 * q:512 * q + 512], B[2 + q][:], AF.Abs, ["pb%d" % (2 + q)], ["ab%d" % q], [2 + q])
        for a, e in DQ:
            if a:
                mm(B[6][32 * a:32 * e, 0:128], T.ib[:, 32 * a:32 * e], T.kc[:], True, False, ["ib", "kc"], 6)
            for k in range(16):
                mm(B[6][32 * a:32 * e, k:128:16], T.ab[:, 512 * a + k:512 * e:16], T.b16[:], False, k == 15,
                   ["ab%d" % q for q in range(a, e)] + ["b16"], 6)
            join(17 if a else 16)
        ts(T.ff[:], T.o3[:], 4096.0, 0.5, OP.is_lt, OP.max, ["o30", "o31"], ["ff"])
        cp(T.nl[:], MN(t, 16, 24), [MNk[t][2]], ["nl"])
        for h in range(2):
            tt(T.e4[:, 64 * h:64 * h + 64], T.ff[:, 64 * h:64 * h + 64], B[h][:, 64:128], OP.mult, ["ff"], ["e4%d" % h], [h])
        tt(T.nme[:], ind(T.iot[:], T.nl[:]), T.e4[:], OP.subtract, IOT + ["nl", "e40", "e41"], ["nme"])
        aff("ev", B[5][:, 256:384], T.e4[:], ["e40", "e41"], ["ev", "pb5"], [5], bias=-4096.0)
        if t < NT - 1:
            ts(T.nx[:, 0:2], MN(t, 16, 18), 2.0, None, OP.mult, None, [MNk[t][2]], ["nx"])
            lists(t + 1)
            repeats(FO, T.fo, "fo", t + 1, 0, 2)
        else:
            decode(1)
        op("V", lambda: V.tensor_tensor_scan(T.pm[:], T.rs[:], B[6][:, 0:128], 0.0, OP.add, OP.min), ["rs"], ["pmin"], [6], dur=128.0)
        cp(T.key[:], B[6][:, 0:128], [], ["key"], [6])
        tt(T.near[:], B[6][:, 0:128], T.tha[:], OP.is_lt, ["tha"], ["near"], [6])
        tt(T.ge[:], ind(T.pm[:], T.bc[:]), T.key[:], OP.is_equal, ["pmin", "bc", "key"], ["ge"])
        w2, plain = (T.w2[:, 0:128], 0.0) if t < NT - 1 else (T.w2[:, 128:256], 2048.0)
        for h, F, fk, bk in ((0, FI, "fi", 1), (1, FO, "fo", 4)):
            mm(B[bk][:, 0:128], w2, F(t, 8, 136), True, False, ["w2", fk + "e%d" % t], bk)
            mm(B[bk][:, 0:128], w2, F(t, 136, 264), False, False, ["w2", fk + "o%d" % t], bk)
            mm(B[bk][:, 0:128], T.near[:], T.nbig[:, 128 * h:128 * h + 128], False, True, ["near", "nbig", "pbig"], bk)
            aff("rr%d" % h, T.rr[:, 128 * h:128 * h + 128], B[bk][:, 0:128], [], ["rr%d" % h], [bk], bias=plain - BIG * h)
        mm(B[0][:, 128:256], T.ge[:], T.ib[:], True, True, ["ge", "ib"], 0)
        tt(T.t1[:], B[0][:, 128:256], T.nme[:], OP.mult, ["nme"], ["t1"], [0])
        tt(T.ep[:], T.t1[:], B[5][:, 256:384], OP.add, ["t1", "ev"], ["ep"], [5])
        if t < NT - 1:
            scat(T.vd, "vd", 0)
            scat(T.pd, "pd", 1)
        else:
            scat(T.ov, "ov", 0)
            scat(T.op_, "op", 1)
        aff("oh", T.oh[:], B[0][:, 128:256], [], ["oh"], [0])
        if LM[1]:
            mm(B[5][:, 0:8], T.ib[:], T.j16[:], True, False, ["ib", "j16"], 5)
            for r in range(16):
                mm(B[5][:, 0:8], T.sk[:, 15 - r:143 - r], T.oh[:, r:128:16], False, r == 15, ["bk", "oh"], 5)
            join(17)
        else:
            mm(B[5][:, 128:256], T.oh[:], T.bk[:], True, True, ["bk", "oh"], 5)
            tt(T.km[:], B[5][:, 128:256], T.mr[:], OP.mult, ["mr"], ["km"], [5])
            mm(B[5][:, 0:8], T.ib[:], T.j16[:], True, False, ["ib", "j16"], 5)
            mm(B[5][:, 0:8], T.km[:], T.b16[:], False, True, ["km", "b16"], 5)
            join(2)
        cp(T.kl[:], B[5][:, 0:8], [], ["kl"], [5])
        tt(T.df[:], ind(T.xg[:], T.kl[:]), ZI(t), OP.subtract, xgk + ["kl", "z%d" % t], ["df"])
        act(ZO(t), T.df[:], AF.Abs, ["df"], ["zo%d" % t])
        aff("z192", T.z192[:], ZI(t), ["z%d" % t], ["z192"], bias=-192.0, f=0.5)
        ts(T.tt[:], T.df[:], 0.5, 191.75, OP.mult, OP.add, ["df"], ["tt"], f=0.5)
        tt(ind(T.xw[:, 0:4096], T.nl[:]), T.tt[:], T.z192[:], OP.add, ["tt", "z192", "nl"], ["xa", "xb"])
        if t < NT - 1:
            tt(ind(T.xw[:, 4096:6144], T.nx[:, 0:2]), T.tt[:, 0:32], T.z192[:, 0:32], OP.add, ["tt", "z192", "nx"], ["xe2"])
            send(ZO(t), [(nxt, ZI(t + 1), T.sem["az%d" % (t + 1)])], ["zo%d" % t], "z%d" % t)
            chain(t + 1)
            mm(B[6][:, 128:256], T.ones[:], T.near[:], True, True, ["ones", "near"], 6)
            act(T.g128[:], B[6][:, 128:256], AF.Identity, [], ["ac0", "g128"], [6], scale=-16.0, acc=T.ac[:, 0:1])
            aff("aq", T.aq[:, 0:1], T.ac[:, 0:1], ["ac0"], ["aq"], scale=1.0 / 4096.0, bias=192.502)
            aff("ac", T.ac[:, 1:2], T.aq[:, 0:1], ["aq", "ac0"], ["ac1"], scale=-4096.0, bias=T.ac[:, 0:1])
            aff("tha", T.tha[:], T.th16[:], ["th16", "ac1"], ["tha"], bias=T.ac[:, 1:2])

    t = NT - 1
    sect[0] = "e"
    dma("Y", T.yz[:], ZO(t), ["zo%d" % t], [], 32)
    dma("Y", T.yvd[:], T.ov[:, 1:1025], ["ov"], [], 512)
    dma("Y", T.ypd[:], T.op_[:, 1:1025], ["op"], [], 512)
    for h, bk in ((0, 1), (1, 4)):
        for i in range(4):
            l = T.ib[:] if i == 0 else T.sc3[:, 128 * i - 128:128 * i]
            mm(B[bk][:], l, T.xw[:, 1024 * i + 512 * h:1024 * i + 512 * h + 512], i == 0, i == 3, ["ib", "sc3", "xa", "xb"], bk)
        act(T.ox[:, 512 * h:512 * h + 512], B[bk][:], AF.Copy, [], ["ox%d" % h], [bk])
        dma("Y", T.yx[:, 512 * h:512 * h + 512], T.ox[:, 512 * h:512 * h + 512], ["ox%d" % h], [], 256)
    cp(T.yl[:], MN(t, 0, 16), [MNk[t][0]], ["yl"])
    ts(T.ya[:], ind(T.iot[:, 0:1536], T.yl[:, 8:16]), 1024.0, -4097.0 * 1025.0, OP.mult, OP.add, ["yl"] + IOT[:3], ["ya"])
    tt(T.yb[:], ind(T.iot[:, 0:1536], T.yl[:, 0:8]), T.ya[:], OP.add, ["yl", "ya"] + IOT[:3], ["yb"])
    dma("Y", T.yvp[:], T.yb[0:128:16, :], ["yb"], [])
    emit(g, T, arrange(ops))
